import numpy as np
import ml_dtypes


def mxq(x, axis, fmt="e4m3"):
    dtype, down = {"e4m3": (ml_dtypes.float8_e4m3fn, 7), "e5m2": (ml_dtypes.float8_e5m2, 14)}[fmt]
    v = np.moveaxis(np.asarray(x, np.float32).astype(ml_dtypes.bfloat16).astype(np.float64), axis, -1)
    blocks = v.reshape(v.shape[:-1] + (-1, 32))
    amax = np.abs(blocks).max(-1, keepdims=True)
    byte = np.maximum(np.where(amax > 0, np.frexp(amax)[1] - 1 + 127, 0) - down, 1)
    scale = np.exp2(byte - 127.0)
    codes = (blocks / scale).astype(np.float32).astype(dtype).astype(np.float64)
    return np.moveaxis((codes * scale).reshape(v.shape), -1, axis)


WIDE = False


def mx_kscale(k):
    if not WIDE:
        return np.ones(k)
    levels = np.array([10, -10, 5, -5, 0])
    if k % 512:
        return np.exp2(np.random.permutation(np.resize(levels, k // 32))).repeat(32)
    a = np.empty((k // 512, 16))
    for p in range(k // 512):
        a[p, :8] = np.random.permutation(np.resize(levels, 8))
        for g in range(8):
            far = levels[np.abs(levels - a[p, g]) >= 10]
            a[p, g + 8] = far[np.random.randint(len(far))]
    return np.exp2(a.ravel()).repeat(32)


def f64(x):
    return np.asarray(x).astype(np.float64)


def striped(idx):
    return np.tile(idx.reshape(-1, 16).T, (8, 1)).astype(np.uint16)


def unstriped(offs):
    return offs[:16].T.reshape(-1).astype(np.int64)


E2M1 = np.array([0.0, 0.5, 1.0, 1.5, 2.0, 3.0, 4.0, 6.0, -0.0, -0.5, -1.0, -1.5, -2.0, -3.0, -4.0, -6.0])


def pack_weight(w, fmt):
    k, n = w.shape
    w = f64(np.asarray(w, np.float32).astype(ml_dtypes.bfloat16)).reshape(k // 32, 32, n)
    amax = np.abs(w).max(1)
    if fmt == "e4m3":
        byte = np.frexp(amax)[1] - 1 + 127 - 7
    else:
        mant, ex = np.frexp(amax / 6.0)
        byte = np.where(mant > 0.5, ex, ex - 1) + 127
    byte = np.clip(np.where(amax > 0, byte, 1), 1, 254)
    scaled = (w * np.exp2(127.0 - byte)[:, None, :]).reshape(k, n).astype(np.float32)
    by_word = np.ascontiguousarray(scaled.reshape(k // 512, 128, 4, n).transpose(0, 1, 3, 2))
    if fmt == "e4m3":
        words = by_word.astype(ml_dtypes.float8_e4m3fn).view(np.uint8)
    else:
        c = by_word.astype(ml_dtypes.float4_e2m1fn).view(np.uint8) & 0xF
        words = (c[..., 0::2] | (c[..., 1::2] << 4)).reshape(k // 512, 128, 2 * n)
    return np.ascontiguousarray(words), np.ascontiguousarray(byte.astype(np.uint8).reshape(k // 512, 16, n))


def unpack_weight(words, scales, fmt):
    g, _, n = scales.shape
    words = np.ascontiguousarray(words).reshape(g, 128, n, -1)
    if fmt == "e4m3":
        vals = words.view(ml_dtypes.float8_e4m3fn).astype(np.float64)
    else:
        nib = np.empty((g, 128, n, 4), np.uint8)
        nib[..., 0::2] = words & 0xF
        nib[..., 1::2] = words >> 4
        vals = E2M1[nib]
    vals = vals * np.repeat(np.exp2(scales.astype(np.float64) - 127.0), 8, axis=1)[..., None]
    return vals.transpose(0, 1, 3, 2).reshape(g * 512, n)


def gelu(v):
    return 0.5 * v * (1.0 + np.tanh(np.sqrt(2.0 / np.pi) * (v + 0.044715 * v**3)))


K, H, N, T, S, P, P2 = 512, 1024, 512, 4096, 2048, 1024, 512

def setup_inputs():
    n = np.random.standard_normal
    s = mx_kscale(K)[:, None]
    u = mx_kscale(H)[:, None]
    tab_words, tab_scales = pack_weight(n((K, T)) * s, "e4m3")
    w2_words, w2_scales = pack_weight(n((K, H)) * 2.0 / np.sqrt(K) / s, "e2m1")
    w4_words, w4_scales = pack_weight(n((H, N)) * 0.8 / np.sqrt(H) / (u * u), "e4m3")
    return {
        "tab_words": tab_words, "tab_scales": tab_scales,
        "offs": striped(np.random.permutation(T)[:S]),
        "pos1": striped(np.random.permutation(S)[:P]),
        "pos2": striped(np.random.permutation(S)[:P]),
        "pos3": striped(np.random.permutation(P)[:P2]),
        "pos4": striped(np.random.permutation(S)[:P2]),
        "w1": (n((K, H)) * 0.8 / np.sqrt(K) / s * u.T).astype(np.float32),
        "w2_words": w2_words, "w2_scales": w2_scales,
        "gain": (np.exp(0.3 * n(H)) * u[:, 0]).astype(np.float32),
        "w3": (n((H, N)) * 1.2 / np.sqrt(H) / (u * u)).astype(np.float32),
        "w4_words": w4_words, "w4_scales": w4_scales,
    }

def reference(tab_words, tab_scales, offs, pos1, pos2, pos3, pos4, w1, w2_words, w2_scales, gain, w3, w4_words, w4_scales):
    v = unpack_weight(tab_words, tab_scales, "e4m3")[:, unstriped(offs)]
    w1q = mxq(f64(w1), 0, "e4m3")
    w2 = unpack_weight(w2_words, w2_scales, "e2m1")
    w3q = mxq(f64(w3), 0, "e4m3")
    w4 = unpack_weight(w4_words, w4_scales, "e4m3")
    h = (w1q.T @ v) + f64(gain)[:, None] * np.tanh(w2.T @ v)
    a1 = np.maximum(h[:, unstriped(pos1)], h[:, unstriped(pos2)])
    a2 = a1[:, unstriped(pos3)] * h[:, unstriped(pos4)]
    a2q = mxq(a2, 0, "e4m3")
    bounded = np.tanh(w3q.T @ a2q)
    plain = w4.T @ a2q
    return np.maximum(bounded, plain)

@@ -1,0 +1,243 @@
+from contextlib import ExitStack
+
+import concourse.mybir as mybir
+
+K, H, N, T, S, PAIRS, KEPT = 512, 1024, 512, 4096, 2048, 1024, 512
+FLOPS = 2 * 2 * K * H * S + 2 * 2 * H * N * KEPT
+
+F32 = mybir.dt.float32
+BF16 = mybir.dt.bfloat16
+I32 = mybir.dt.int32
+U32 = mybir.dt.uint32
+U16 = mybir.dt.uint16
+U8 = mybir.dt.uint8
+FP8X4 = mybir.dt.float8_e4m3fn_x4
+FP4X4 = mybir.dt.float4_e2m1fn_x4
+ALU = mybir.AluOpType
+ACT = mybir.ActivationFunctionType
+
+P = 128
+PACK = 4
+BANK = 512
+CHUNKS = S // BANK
+SLICES = H // P
+PASSES = H // (P * PACK)
+OUT_TILES = N // P
+
+
+def tile_list_laundering_alert_scores_kernel(
+    tc, tab_words, tab_scales, offs, pos1, pos2, pos3, pos4, w1, w2_words, w2_scales, gain, w3, w4_words, w4_scales, out
+):
+    nc = tc.nc
+    with ExitStack() as ctx:
+        keep = ctx.enter_context(tc.tile_pool(name="keep", bufs=1))
+        ring = ctx.enter_context(tc.tile_pool(name="ring", bufs=2))
+        psum = ctx.enter_context(tc.psum_pool(name="psum", bufs=1))
+
+        def load_list(source, name):
+            t = keep.tile(list(source.shape), U16, name=name)
+            nc.sync.dma_start(t[:], source)
+            return t
+
+        tab_b = keep.tile([P, T], U8, align_bytes=64)
+        nc.vector.memset(tab_b[:].bitcast(I32), 0)
+        w2_b_raw = keep.tile([P, H], U8, align_bytes=64)
+        nc.gpsimd.memset(w2_b_raw[:].bitcast(I32), 0)
+        w4_b = keep.tile([P, PASSES * N], U8, align_bytes=64)
+        nc.gpsimd.memset(w4_b[:].bitcast(I32), 0)
+
+        idx = load_list(offs, "idx")
+        for q in range(4):
+            nc.scalar.dma_start(tab_b[32 * q : 32 * q + 4, :].bitcast(I32), tab_scales[0, 4 * q : 4 * q + 4, :].bitcast(I32))
+        for q in range(4):
+            nc.gpsimd.dma_start(w2_b_raw[32 * q : 32 * q + 4, :].bitcast(I32), w2_scales[0, 4 * q : 4 * q + 4, :].bitcast(I32))
+        tab_w = keep.tile([P, T], I32, align_bytes=64)
+        nc.sync.dma_start(tab_w[:], tab_words[0].rearrange("p t i -> p (t i)").bitcast(I32))
+        w1_raw = []
+        for b in range(PASSES):
+            w1_raw.append(keep.tile([P, PACK, BANK], F32, name="w1_raw%d" % b))
+        w1_rows = w1.rearrange("(p j) c -> p j c", j=PACK)
+        nc.sync.dma_start(w1_raw[0][:], w1_rows[:, :, 0:BANK])
+        w2_w_raw = keep.tile([P, H // 2], I32, align_bytes=64)
+        nc.sync.dma_start(w2_w_raw[:], w2_words[0].bitcast(I32))
+        p1 = load_list(pos1, "p1")
+        p2 = load_list(pos2, "p2")
+        p4 = load_list(pos4, "p4")
+        p3 = load_list(pos3, "p3")
+        gain_sb = keep.tile([P, PASSES, PACK], F32)
+        nc.sync.dma_start(gain_sb[:], gain.rearrange("(b p t) -> p b t", p=P, t=PACK))
+        nc.sync.dma_start(w1_raw[1][:], w1_rows[:, :, BANK : 2 * BANK])
+        w3_raw = []
+        for a in range(PASSES):
+            w3_raw.append(keep.tile([P, PACK, N], F32, name="w3_raw%d" % a))
+            nc.sync.dma_start(w3_raw[a][:], w3[512 * a : 512 * (a + 1), :].rearrange("(p j) c -> p j c", j=PACK))
+        w4_w = keep.tile([P, PASSES, N], I32, align_bytes=64)
+        nc.sync.dma_start(w4_w[:], w4_words.rearrange("a p c i -> p a (c i)").bitcast(I32))
+        for q in range(4):
+            nc.sync.dma_start(
+                w4_b[32 * q : 32 * q + 4, :].bitcast(I32).rearrange("r (a c) -> r a c", a=PASSES),
+                w4_scales[:, 4 * q : 4 * q + 4, :].bitcast(I32).rearrange("a r c -> r a c"),
+            )
+
+        v_b = keep.tile([P, S], U8, align_bytes=64)
+        v_w = keep.tile([P, S], U32, align_bytes=64)
+        for c in range(2):
+            nc.vector.tensor_copy(v_b[:, c * 1024 : (c + 1) * 1024], tab_b[:].indirect(idx[:, c * 64 : (c + 1) * 64]))
+
+        def gather_words(c):
+            nc.vector.tensor_copy(
+                v_w[:, c * BANK : (c + 1) * BANK], tab_w[:].bitcast(U32).indirect(idx[:, c * 32 : (c + 1) * 32])
+            )
+
+        w2_w = keep.tile([P, 2 * H], U8, align_bytes=64)
+        nc.scalar.copy(
+            w2_w[:].bitcast(U16).rearrange("p (b t m) -> p b t m", b=PASSES, t=PACK),
+            w2_w_raw[:].bitcast(U16).rearrange("p (b m t) -> p b t m", b=PASSES, t=PACK),
+        )
+        w2_b = keep.tile([P, H], U8, align_bytes=64)
+        nc.gpsimd.tensor_copy(
+            w2_b[:].rearrange("p (b t m) -> p b t m", b=PASSES, t=PACK),
+            w2_b_raw[:].rearrange("p (b m t) -> p b t m", b=PASSES, t=PACK),
+        )
+
+        w1_w = keep.tile([P, H], U32, align_bytes=64)
+        w1_b = keep.tile([P, H], U8, align_bytes=64)
+        w1_bf = {}
+
+        def cast_w1(s):
+            b, t = divmod(s, PACK)
+            w1_bf[s] = ring.tile([P, P, PACK], BF16, name="w1_bf", align_bytes=64)
+            nc.scalar.copy(w1_bf[s][:], w1_raw[b][:].rearrange("p j (m t) -> p t m j", t=PACK)[:, t, :, :])
+
+        def quant_w1(s):
+            cols = slice(s * P, (s + 1) * P)
+            nc.vector.quantize_mx(
+                out=w1_w[:, cols].bitcast(FP8X4), scales=w1_b[:, cols], in_=w1_bf[s][:].rearrange("p m j -> p (m j)")
+            )
+
+        def interleave(engine_copy, dst, src):
+            engine_copy(dst.rearrange("p (c i) t -> p c t i", i=4), src.rearrange("p t (c i) -> p c t i", i=4))
+
+        h = {}
+        th = {}
+        lin = {}
+
+        def stage1(s, c):
+            cols = slice(s * P, (s + 1) * P)
+            toks = slice(c * BANK, (c + 1) * BANK)
+            arg = psum.tile([P, BANK], F32, name="arg", tag="bank%d" % (2 * c))
+            nc.tensor.matmul_mx(
+                out=arg[:], lhsT=w2_w[:, 2 * s * P : 2 * (s + 1) * P].bitcast(FP4X4), lhsT_scale=w2_b[:, cols],
+                rhs=v_w[:, toks].bitcast(FP8X4), rhs_scale=v_b[:, toks], start=True, stop=True,
+            )
+            lin[s, c] = psum.tile([P, BANK], F32, name="lin", tag="bank%d" % (2 * c + 1))
+            nc.tensor.matmul_mx(
+                out=lin[s, c][:], lhsT=w1_w[:, cols].bitcast(FP8X4), lhsT_scale=w1_b[:, cols],
+                rhs=v_w[:, toks].bitcast(FP8X4), rhs_scale=v_b[:, toks], start=True, stop=True,
+            )
+            th[s, c] = ring.tile([P, BANK], F32, name="th", bufs=4)
+            nc.scalar.activation(th[s, c][:], arg[:], ACT.Tanh)
+
+        def combine(s, c):
+            b, t = divmod(s, PACK)
+            if c == 0:
+                h[s] = ring.tile([P, S], F32, name="h")
+            nc.vector.scalar_tensor_tensor(
+                out=h[s][:, c * BANK : (c + 1) * BANK], in0=th[s, c][:], scalar=gain_sb[:, b, t : t + 1],
+                in1=lin[s, c][:], op0=ALU.mult, op1=ALU.add,
+            )
+
+        w3_w = keep.tile([P, PASSES * N], U32, align_bytes=64)
+        w3_b = keep.tile([P, PASSES * N], U8, align_bytes=64)
+        a2_w = keep.tile([P, PASSES * KEPT], U32, align_bytes=64)
+        a2_b = keep.tile([P, PASSES * KEPT], U8, align_bytes=64)
+
+        def quantize(words, planes, a, src):
+            cols = slice(a * BANK, (a + 1) * BANK)
+            nc.vector.quantize_mx(
+                out=words[:, cols].bitcast(FP8X4), scales=planes[:, cols], in_=src[:].rearrange("p c t -> p (c t)")
+            )
+
+        bounded = {}
+        plain = {}
+
+        def stage2(a, o):
+            cols = slice(a * N + o * P, a * N + (o + 1) * P)
+            toks = slice(a * KEPT, (a + 1) * KEPT)
+            if a == 0:
+                bounded[o] = psum.tile([P, KEPT], F32, name="bounded", tag="bank%d" % (2 * o))
+                plain[o] = psum.tile([P, KEPT], F32, name="plain", tag="bank%d" % (2 * o + 1))
+            nc.tensor.matmul_mx(
+                out=bounded[o][:], lhsT=w3_w[:, cols].bitcast(FP8X4), lhsT_scale=w3_b[:, cols],
+                rhs=a2_w[:, toks].bitcast(FP8X4), rhs_scale=a2_b[:, toks], start=(a == 0), stop=(a == PASSES - 1),
+            )
+            nc.tensor.matmul_mx(
+                out=plain[o][:], lhsT=w4_w[:, a, o * P : (o + 1) * P].bitcast(FP8X4), lhsT_scale=w4_b[:, cols],
+                rhs=a2_w[:, toks].bitcast(FP8X4), rhs_scale=a2_b[:, toks], start=(a == 0), stop=(a == PASSES - 1),
+            )
+
+        cast_w1(0)
+        cast_w1(1)
+        gather_words(0)
+        quant_w1(0)
+        gather_words(1)
+        stage1(0, 0)
+        stage1(0, 1)
+        gather_words(2)
+        stage1(0, 2)
+        combine(0, 0)
+        gather_words(3)
+        stage1(0, 3)
+        quant_w1(1)
+        for c in range(1, CHUNKS):
+            combine(0, c)
+
+        a2_f32 = {}
+        a2_bf = {}
+        w3_bf = {}
+        for s in range(SLICES):
+            a, t = divmod(s, PACK)
+            last = s == SLICES - 1
+            if not last:
+                for c in range(CHUNKS):
+                    stage1(s + 1, c)
+            else:
+                for o in range(OUT_TILES):
+                    stage2(0, o)
+            if s + 2 < SLICES:
+                cast_w1(s + 2)
+            if s in (1, 2):
+                w3_bf[s - 1] = ring.tile([P, N, PACK], BF16, name="w3_bf", align_bytes=64)
+                interleave(nc.scalar.copy, w3_bf[s - 1][:], w3_raw[s - 1][:])
+            g1 = ring.tile([P, PAIRS], F32, name="g1")
+            nc.vector.tensor_copy(g1[:], h[s][:].indirect(p1[:]))
+            g2 = ring.tile([P, PAIRS], F32, name="g2")
+            nc.vector.tensor_copy(g2[:], h[s][:].indirect(p2[:]))
+            g4 = ring.tile([P, KEPT], F32, name="g4")
+            nc.vector.tensor_copy(g4[:], h[s][:].indirect(p4[:]))
+            a1 = ring.tile([P, PAIRS], F32, name="a1")
+            nc.vector.tensor_tensor(a1[:], g1[:], g2[:], ALU.max)
+            if s + 2 < SLICES:
+                quant_w1(s + 2)
+            if s in (2, 3):
+                quantize(w3_w, w3_b, s - 2, w3_bf[s - 2])
+            if s == PACK:
+                quantize(a2_w, a2_b, 0, a2_bf[0])
+            if not last:
+                for c in range(CHUNKS):
+                    combine(s + 1, c)
+            if t == 0:
+                a2_f32[a] = ring.tile([P, PACK, KEPT], F32, name="a2_f32")
+            nc.vector.tensor_tensor(a2_f32[a][:, t, :], a1[:].indirect(p3[:]), g4[:], ALU.mult)
+            if t == PACK - 1:
+                a2_bf[a] = ring.tile([P, KEPT, PACK], BF16, name="a2_bf", align_bytes=64)
+                interleave(nc.vector.tensor_copy if last else nc.scalar.copy, a2_bf[a][:], a2_f32[a][:])
+
+        quantize(a2_w, a2_b, 1, a2_bf[1])
+        for o in range(OUT_TILES):
+            stage2(1, o)
+            tb = ring.tile([P, KEPT], F32, name="tb")
+            nc.scalar.activation(tb[:], bounded[o][:], ACT.Tanh)
+            res = ring.tile([P, KEPT], F32, name="res", bufs=4)
+            nc.vector.tensor_tensor(res[:], plain[o][:], tb[:], ALU.max)
+            nc.sync.dma_start(out[o * P : (o + 1) * P, :], res[:])

@@ -39,7 +39,7 @@ def tile_list_laundering_alert_scores_kernel(
             nc.sync.dma_start(t[:], source)
             return t
 
-        tab_b = keep.tile([P, T], U8, align_bytes=64)
+        tab_b = keep.tile([P, T], U8, tag="scales_then_words", align_bytes=64)
         nc.vector.memset(tab_b[:].bitcast(I32), 0)
         w2_b_raw = keep.tile([P, H], U8, align_bytes=64)
         nc.gpsimd.memset(w2_b_raw[:].bitcast(I32), 0)
@@ -51,21 +51,21 @@ def tile_list_laundering_alert_scores_kernel(
             nc.scalar.dma_start(tab_b[32 * q : 32 * q + 4, :].bitcast(I32), tab_scales[0, 4 * q : 4 * q + 4, :].bitcast(I32))
         for q in range(4):
             nc.gpsimd.dma_start(w2_b_raw[32 * q : 32 * q + 4, :].bitcast(I32), w2_scales[0, 4 * q : 4 * q + 4, :].bitcast(I32))
-        tab_w = keep.tile([P, T], I32, align_bytes=64)
-        nc.sync.dma_start(tab_w[:], tab_words[0].rearrange("p t i -> p (t i)").bitcast(I32))
+        p1 = load_list(pos1, "p1")
+        p2 = load_list(pos2, "p2")
         w1_raw = []
         for b in range(PASSES):
             w1_raw.append(keep.tile([P, PACK, BANK], F32, name="w1_raw%d" % b))
         w1_rows = w1.rearrange("(p j) c -> p j c", j=PACK)
-        nc.sync.dma_start(w1_raw[0][:], w1_rows[:, :, 0:BANK])
         w2_w_raw = keep.tile([P, H // 2], I32, align_bytes=64)
+        nc.sync.dma_start(w1_raw[0][:], w1_rows[:, :, 0:BANK])
         nc.sync.dma_start(w2_w_raw[:], w2_words[0].bitcast(I32))
-        p1 = load_list(pos1, "p1")
-        p2 = load_list(pos2, "p2")
-        p4 = load_list(pos4, "p4")
-        p3 = load_list(pos3, "p3")
+        tab_w = keep.tile([P, T], I32, align_bytes=64)
+        nc.sync.dma_start(tab_w[:], tab_words[0].rearrange("p t i -> p (t i)").bitcast(I32))
         gain_sb = keep.tile([P, PASSES, PACK], F32)
         nc.sync.dma_start(gain_sb[:], gain.rearrange("(b p t) -> p b t", p=P, t=PACK))
+        p3 = load_list(pos3, "p3")
+        p4 = load_list(pos4, "p4")
         nc.sync.dma_start(w1_raw[1][:], w1_rows[:, :, BANK : 2 * BANK])
         w3_raw = []
         for a in range(PASSES):
@@ -80,9 +80,10 @@ def tile_list_laundering_alert_scores_kernel(
             )
 
         v_b = keep.tile([P, S], U8, align_bytes=64)
-        v_w = keep.tile([P, S], U32, align_bytes=64)
         for c in range(2):
             nc.vector.tensor_copy(v_b[:, c * 1024 : (c + 1) * 1024], tab_b[:].indirect(idx[:, c * 64 : (c + 1) * 64]))
+
+        v_w = keep.tile([P, S], U32, tag="scales_then_words", align_bytes=64)
 
         def gather_words(c):
             nc.vector.tensor_copy(
@@ -100,140 +101,164 @@ def tile_list_laundering_alert_scores_kernel(
             w2_b_raw[:].rearrange("p (b m t) -> p b t m", b=PASSES, t=PACK),
         )
 
-        w1_w = keep.tile([P, H], U32, align_bytes=64)
-        w1_b = keep.tile([P, H], U8, align_bytes=64)
-        w1_bf = {}
-
-        def cast_w1(s):
-            b, t = divmod(s, PACK)
-            w1_bf[s] = ring.tile([P, P, PACK], BF16, name="w1_bf", align_bytes=64)
-            nc.scalar.copy(w1_bf[s][:], w1_raw[b][:].rearrange("p j (m t) -> p t m j", t=PACK)[:, t, :, :])
-
-        def quant_w1(s):
-            cols = slice(s * P, (s + 1) * P)
-            nc.vector.quantize_mx(
-                out=w1_w[:, cols].bitcast(FP8X4), scales=w1_b[:, cols], in_=w1_bf[s][:].rearrange("p m j -> p (m j)")
-            )
-
         def interleave(engine_copy, dst, src):
             engine_copy(dst.rearrange("p (c i) t -> p c t i", i=4), src.rearrange("p t (c i) -> p c t i", i=4))
+
+        def quantize(src, name, tag):
+            words = keep.tile([P, BANK], U32, name=name + "_w", tag=tag, align_bytes=64)
+            planes = keep.tile([P, BANK], U8, name=name + "_b", align_bytes=64)
+            nc.vector.quantize_mx(out=words[:].bitcast(FP8X4), scales=planes[:], in_=src)
+            return words, planes
+
+        def deal_w1(dst, b, t0, t1):
+            nc.scalar.copy(dst[:, t0:t1, :, :], w1_raw[b][:].rearrange("p j (m t) -> p t m j", t=PACK)[:, t0:t1, :, :])
+
+        w1_q = {}
+        w1_bf = []
+        for b in range(PASSES):
+            w1_bf.append(keep.tile([P, PACK, P, PACK], BF16, name="w1_bf%d" % b, align_bytes=64))
 
         h = {}
         th = {}
         lin = {}
+        off_th = {}
+        off_lin = {}
+        off_term = {}
 
-        def stage1(s, c):
-            cols = slice(s * P, (s + 1) * P)
-            toks = slice(c * BANK, (c + 1) * BANK)
-            arg = psum.tile([P, BANK], F32, name="arg", tag="bank%d" % (2 * c))
-            nc.tensor.matmul_mx(
-                out=arg[:], lhsT=w2_w[:, 2 * s * P : 2 * (s + 1) * P].bitcast(FP4X4), lhsT_scale=w2_b[:, cols],
-                rhs=v_w[:, toks].bitcast(FP8X4), rhs_scale=v_b[:, toks], start=True, stop=True,
-            )
-            lin[s, c] = psum.tile([P, BANK], F32, name="lin", tag="bank%d" % (2 * c + 1))
-            nc.tensor.matmul_mx(
-                out=lin[s, c][:], lhsT=w1_w[:, cols].bitcast(FP8X4), lhsT_scale=w1_b[:, cols],
-                rhs=v_w[:, toks].bitcast(FP8X4), rhs_scale=v_b[:, toks], start=True, stop=True,
-            )
-            th[s, c] = ring.tile([P, BANK], F32, name="th", bufs=4)
-            nc.scalar.activation(th[s, c][:], arg[:], ACT.Tanh)
+        def on_vector(s):
+            return CHUNKS if s < 2 else 1
 
-        def combine(s, c):
+        def stage1(s):
             b, t = divmod(s, PACK)
-            if c == 0:
-                h[s] = ring.tile([P, S], F32, name="h")
-            nc.vector.scalar_tensor_tensor(
-                out=h[s][:, c * BANK : (c + 1) * BANK], in0=th[s, c][:], scalar=gain_sb[:, b, t : t + 1],
-                in1=lin[s, c][:], op0=ALU.mult, op1=ALU.add,
-            )
+            cols = slice(s * P, (s + 1) * P)
+            w1_words, w1_planes = w1_q[b]
+            nv = on_vector(s)
+            if nv < CHUNKS:
+                off_th[s] = ring.tile([P, (CHUNKS - nv) * BANK], F32, name="off_th", bufs=1)
+                off_lin[s] = ring.tile([P, (CHUNKS - nv) * BANK], F32, name="off_lin")
+                off_term[s] = ring.tile([P, (CHUNKS - nv) * BANK], F32, name="off_term")
+            for c in range(CHUNKS):
+                toks = slice(c * BANK, (c + 1) * BANK)
+                arg = psum.tile([P, BANK], F32, name="arg", tag="bank%d" % (2 * c))
+                nc.tensor.matmul_mx(
+                    out=arg[:], lhsT=w2_w[:, 2 * s * P : 2 * (s + 1) * P].bitcast(FP4X4), lhsT_scale=w2_b[:, cols],
+                    rhs=v_w[:, toks].bitcast(FP8X4), rhs_scale=v_b[:, toks], start=True, stop=True,
+                )
+                lin[s, c] = psum.tile([P, BANK], F32, name="lin", tag="bank%d" % (2 * c + 1))
+                nc.tensor.matmul_mx(
+                    out=lin[s, c][:], lhsT=w1_words[:, t * P : (t + 1) * P].bitcast(FP8X4),
+                    lhsT_scale=w1_planes[:, t * P : (t + 1) * P],
+                    rhs=v_w[:, toks].bitcast(FP8X4), rhs_scale=v_b[:, toks], start=True, stop=True,
+                )
+                if c < nv:
+                    th[s, c] = ring.tile([P, BANK], F32, name="th", bufs=4)
+                    nc.scalar.activation(th[s, c][:], arg[:], ACT.Tanh)
+                else:
+                    part = slice((c - nv) * BANK, (c - nv + 1) * BANK)
+                    nc.scalar.activation(off_th[s][:, part], arg[:], ACT.Tanh)
+                    nc.scalar.copy(off_lin[s][:, part], lin[s, c][:])
+            if nv < CHUNKS:
+                nc.scalar.activation(off_term[s][:], off_th[s][:], ACT.Copy, scale=gain_sb[:, b, t : t + 1])
 
-        w3_w = keep.tile([P, PASSES * N], U32, align_bytes=64)
-        w3_b = keep.tile([P, PASSES * N], U8, align_bytes=64)
-        a2_w = keep.tile([P, PASSES * KEPT], U32, align_bytes=64)
-        a2_b = keep.tile([P, PASSES * KEPT], U8, align_bytes=64)
+        def open_h(s):
+            h[s] = ring.tile([P, S], F32, name="h")
+            nv = on_vector(s)
+            if nv < CHUNKS:
+                nc.gpsimd.tensor_tensor(h[s][:, nv * BANK :], off_lin[s][:], off_term[s][:], ALU.add)
 
-        def quantize(words, planes, a, src):
-            cols = slice(a * BANK, (a + 1) * BANK)
-            nc.vector.quantize_mx(
-                out=words[:, cols].bitcast(FP8X4), scales=planes[:, cols], in_=src[:].rearrange("p c t -> p (c t)")
-            )
+        def combine(s):
+            b, t = divmod(s, PACK)
+            for c in range(on_vector(s)):
+                nc.vector.scalar_tensor_tensor(
+                    out=h[s][:, c * BANK : (c + 1) * BANK], in0=th[s, c][:], scalar=gain_sb[:, b, t : t + 1],
+                    in1=lin[s, c][:], op0=ALU.mult, op1=ALU.add,
+                )
 
+        w3_q = {}
+        a2_q = {}
         bounded = {}
         plain = {}
 
         def stage2(a, o):
-            cols = slice(a * N + o * P, a * N + (o + 1) * P)
-            toks = slice(a * KEPT, (a + 1) * KEPT)
+            cols = slice(o * P, (o + 1) * P)
             if a == 0:
                 bounded[o] = psum.tile([P, KEPT], F32, name="bounded", tag="bank%d" % (2 * o))
                 plain[o] = psum.tile([P, KEPT], F32, name="plain", tag="bank%d" % (2 * o + 1))
             nc.tensor.matmul_mx(
-                out=bounded[o][:], lhsT=w3_w[:, cols].bitcast(FP8X4), lhsT_scale=w3_b[:, cols],
-                rhs=a2_w[:, toks].bitcast(FP8X4), rhs_scale=a2_b[:, toks], start=(a == 0), stop=(a == PASSES - 1),
+                out=bounded[o][:], lhsT=w3_q[a][0][:, cols].bitcast(FP8X4), lhsT_scale=w3_q[a][1][:, cols],
+                rhs=a2_q[a][0][:].bitcast(FP8X4), rhs_scale=a2_q[a][1][:], start=(a == 0), stop=(a == PASSES - 1),
             )
             nc.tensor.matmul_mx(
-                out=plain[o][:], lhsT=w4_w[:, a, o * P : (o + 1) * P].bitcast(FP8X4), lhsT_scale=w4_b[:, cols],
-                rhs=a2_w[:, toks].bitcast(FP8X4), rhs_scale=a2_b[:, toks], start=(a == 0), stop=(a == PASSES - 1),
+                out=plain[o][:], lhsT=w4_w[:, a, cols].bitcast(FP8X4), lhsT_scale=w4_b[:, a * N + o * P : a * N + (o + 1) * P],
+                rhs=a2_q[a][0][:].bitcast(FP8X4), rhs_scale=a2_q[a][1][:], start=(a == 0), stop=(a == PASSES - 1),
             )
 
-        cast_w1(0)
-        cast_w1(1)
-        gather_words(0)
-        quant_w1(0)
-        gather_words(1)
-        stage1(0, 0)
-        stage1(0, 1)
-        gather_words(2)
-        stage1(0, 2)
-        combine(0, 0)
-        gather_words(3)
-        stage1(0, 3)
-        quant_w1(1)
-        for c in range(1, CHUNKS):
-            combine(0, c)
+        def flat(tile4):
+            return tile4[:].rearrange("p t m j -> p (t m j)")
+
+        def flat3(tile3):
+            return tile3[:].rearrange("p c t -> p (c t)")
+
+        deal_w1(w1_bf[0], 0, 0, PACK)
+        w1_q[0] = quantize(flat(w1_bf[0]), "w1a", "w1a_w")
+        for c in range(CHUNKS):
+            gather_words(c)
+        stage1(0)
+        open_h(0)
+        combine(0)
+        deal_w1(w1_bf[1], 1, 0, PACK)
+        stage1(1)
+        open_h(1)
 
         a2_f32 = {}
         a2_bf = {}
         w3_bf = {}
+        HALF = PAIRS // 2
+        QUART = KEPT // 2
         for s in range(SLICES):
             a, t = divmod(s, PACK)
             last = s == SLICES - 1
             if not last:
-                for c in range(CHUNKS):
-                    stage1(s + 1, c)
-            else:
-                for o in range(OUT_TILES):
-                    stage2(0, o)
-            if s + 2 < SLICES:
-                cast_w1(s + 2)
+                combine(s + 1)
             if s in (1, 2):
                 w3_bf[s - 1] = ring.tile([P, N, PACK], BF16, name="w3_bf", align_bytes=64)
                 interleave(nc.scalar.copy, w3_bf[s - 1][:], w3_raw[s - 1][:])
-            g1 = ring.tile([P, PAIRS], F32, name="g1")
+            if s == PACK:
+                a2_bf[0] = ring.tile([P, KEPT, PACK], BF16, name="a2_bf", align_bytes=64)
+                interleave(nc.scalar.copy, a2_bf[0][:], a2_f32[0][:])
+            if s + 2 < SLICES:
+                stage1(s + 2)
+            g1 = keep.tile([P, PAIRS], F32, name="g1", tag="g1_%d" % s if s in (1, 3, 4, 7) else "g1", align_bytes=64)
             nc.vector.tensor_copy(g1[:], h[s][:].indirect(p1[:]))
             g2 = ring.tile([P, PAIRS], F32, name="g2")
-            nc.vector.tensor_copy(g2[:], h[s][:].indirect(p2[:]))
-            g4 = ring.tile([P, KEPT], F32, name="g4")
-            nc.vector.tensor_copy(g4[:], h[s][:].indirect(p4[:]))
+            for u in range(2):
+                nc.vector.tensor_copy(g2[:, u * HALF : (u + 1) * HALF], h[s][:].indirect(p2[:, u * 32 : (u + 1) * 32]))
             a1 = ring.tile([P, PAIRS], F32, name="a1")
-            nc.vector.tensor_tensor(a1[:], g1[:], g2[:], ALU.max)
-            if s + 2 < SLICES:
-                quant_w1(s + 2)
-            if s in (2, 3):
-                quantize(w3_w, w3_b, s - 2, w3_bf[s - 2])
-            if s == PACK:
-                quantize(a2_w, a2_b, 0, a2_bf[0])
-            if not last:
-                for c in range(CHUNKS):
-                    combine(s + 1, c)
+            for u in range(2):
+                part = slice(u * HALF, (u + 1) * HALF)
+                nc.vector.tensor_tensor(a1[:, part], g1[:, part], g2[:, part], ALU.max)
+            if s == 1:
+                w1_q[1] = quantize(flat(w1_bf[1]), "w1b", "g1_%d" % s)
+            if s in (3, 4):
+                w3_q[s - 3] = quantize(flat3(w3_bf[s - 3]), "w3_%d" % (s - 3), "g1_%d" % s)
+            if last:
+                a2_q[0] = quantize(flat3(a2_bf[0]), "a2_0", "g1_%d" % s)
+                for o in range(OUT_TILES):
+                    stage2(0, o)
+            g3 = ring.tile([P, KEPT], F32, name="g3")
+            for u in range(2):
+                nc.vector.tensor_copy(g3[:, u * QUART : (u + 1) * QUART], a1[:].indirect(p3[:, u * 16 : (u + 1) * 16]))
             if t == 0:
                 a2_f32[a] = ring.tile([P, PACK, KEPT], F32, name="a2_f32")
-            nc.vector.tensor_tensor(a2_f32[a][:, t, :], a1[:].indirect(p3[:]), g4[:], ALU.mult)
-            if t == PACK - 1:
-                a2_bf[a] = ring.tile([P, KEPT, PACK], BF16, name="a2_bf", align_bytes=64)
-                interleave(nc.vector.tensor_copy if last else nc.scalar.copy, a2_bf[a][:], a2_f32[a][:])
+            for u in range(2):
+                part = slice(u * QUART, (u + 1) * QUART)
+                nc.vector.tensor_tensor(a2_f32[a][:, t, part], h[s][:].indirect(p4[:, u * 16 : (u + 1) * 16]), g3[:, part], ALU.mult)
+            if s + 2 < SLICES:
+                open_h(s + 2)
 
-        quantize(a2_w, a2_b, 1, a2_bf[1])
+        a2_bf[1] = ring.tile([P, KEPT, PACK], BF16, name="a2_bf", align_bytes=64)
+        interleave(nc.vector.tensor_copy, a2_bf[1][:], a2_f32[1][:])
+        a2_q[1] = quantize(flat3(a2_bf[1]), "a2_1", "a2_1_w")
         for o in range(OUT_TILES):
             stage2(1, o)
             tb = ring.tile([P, KEPT], F32, name="tb")

@@ -42,35 +42,31 @@ def tile_list_laundering_alert_scores_kernel(
         tab_b = keep.tile([P, T], U8, tag="scales_then_words", align_bytes=64)
         nc.vector.memset(tab_b[:].bitcast(I32), 0)
         w2_b_raw = keep.tile([P, H], U8, align_bytes=64)
-        nc.gpsimd.memset(w2_b_raw[:].bitcast(I32), 0)
+        nc.vector.memset(w2_b_raw[:].bitcast(I32), 0)
         w4_b = keep.tile([P, PASSES * N], U8, align_bytes=64)
         nc.gpsimd.memset(w4_b[:].bitcast(I32), 0)
 
         idx = load_list(offs, "idx")
         for q in range(4):
             nc.scalar.dma_start(tab_b[32 * q : 32 * q + 4, :].bitcast(I32), tab_scales[0, 4 * q : 4 * q + 4, :].bitcast(I32))
-        for q in range(4):
-            nc.gpsimd.dma_start(w2_b_raw[32 * q : 32 * q + 4, :].bitcast(I32), w2_scales[0, 4 * q : 4 * q + 4, :].bitcast(I32))
         p1 = load_list(pos1, "p1")
         p2 = load_list(pos2, "p2")
+        p3 = load_list(pos3, "p3")
         w1_raw = []
         for b in range(PASSES):
-            w1_raw.append(keep.tile([P, PACK, BANK], F32, name="w1_raw%d" % b))
+            w1_raw.append(keep.tile([P, PACK, BANK], F32, name="w1_raw%d" % b, tag="raw%d" % b))
         w1_rows = w1.rearrange("(p j) c -> p j c", j=PACK)
         w2_w_raw = keep.tile([P, H // 2], I32, align_bytes=64)
         nc.sync.dma_start(w1_raw[0][:], w1_rows[:, :, 0:BANK])
         nc.sync.dma_start(w2_w_raw[:], w2_words[0].bitcast(I32))
         tab_w = keep.tile([P, T], I32, align_bytes=64)
-        nc.sync.dma_start(tab_w[:], tab_words[0].rearrange("p t i -> p (t i)").bitcast(I32))
+        nc.sync.dma_start(tab_w[:], tab_words[0].rearrange("p t i -> p (t i)").bitcast(I32), max_dma_last_dim=4096)
+        for q in range(4):
+            nc.scalar.dma_start(w2_b_raw[32 * q : 32 * q + 4, :].bitcast(I32), w2_scales[0, 4 * q : 4 * q + 4, :].bitcast(I32))
         gain_sb = keep.tile([P, PASSES, PACK], F32)
         nc.sync.dma_start(gain_sb[:], gain.rearrange("(b p t) -> p b t", p=P, t=PACK))
-        p3 = load_list(pos3, "p3")
         p4 = load_list(pos4, "p4")
         nc.sync.dma_start(w1_raw[1][:], w1_rows[:, :, BANK : 2 * BANK])
-        w3_raw = []
-        for a in range(PASSES):
-            w3_raw.append(keep.tile([P, PACK, N], F32, name="w3_raw%d" % a))
-            nc.sync.dma_start(w3_raw[a][:], w3[512 * a : 512 * (a + 1), :].rearrange("(p j) c -> p j c", j=PACK))
         w4_w = keep.tile([P, PASSES, N], I32, align_bytes=64)
         nc.sync.dma_start(w4_w[:], w4_words.rearrange("a p c i -> p a (c i)").bitcast(I32))
         for q in range(4):
@@ -96,47 +92,50 @@ def tile_list_laundering_alert_scores_kernel(
             w2_w_raw[:].bitcast(U16).rearrange("p (b m t) -> p b t m", b=PASSES, t=PACK),
         )
         w2_b = keep.tile([P, H], U8, align_bytes=64)
-        nc.gpsimd.tensor_copy(
-            w2_b[:].rearrange("p (b t m) -> p b t m", b=PASSES, t=PACK),
-            w2_b_raw[:].rearrange("p (b m t) -> p b t m", b=PASSES, t=PACK),
-        )
+        w2_b_dealt = w2_b[:].rearrange("p (b t m) -> p b t m", b=PASSES, t=PACK)
+        w2_b_given = w2_b_raw[:].rearrange("p (b m t) -> p b t m", b=PASSES, t=PACK)
+        for b, t0, t1 in ((0, 0, 1), (0, 1, PACK), (1, 0, PACK)):
+            nc.gpsimd.tensor_copy(w2_b_dealt[:, b, t0:t1, :], w2_b_given[:, b, t0:t1, :])
 
         def interleave(engine_copy, dst, src):
             engine_copy(dst.rearrange("p (c i) t -> p c t i", i=4), src.rearrange("p t (c i) -> p c t i", i=4))
 
-        def quantize(src, name, tag):
-            words = keep.tile([P, BANK], U32, name=name + "_w", tag=tag, align_bytes=64)
-            planes = keep.tile([P, BANK], U8, name=name + "_b", align_bytes=64)
-            nc.vector.quantize_mx(out=words[:].bitcast(FP8X4), scales=planes[:], in_=src)
+        def mx_tiles(name, width, tag):
+            words = keep.tile([P, width], U32, name=name + "_w", tag=tag, align_bytes=64)
+            planes = keep.tile([P, width], U8, name=name + "_b", align_bytes=64)
             return words, planes
 
-        def deal_w1(dst, b, t0, t1):
-            nc.scalar.copy(dst[:, t0:t1, :, :], w1_raw[b][:].rearrange("p j (m t) -> p t m j", t=PACK)[:, t0:t1, :, :])
+        def quantize(pair, cols, src):
+            nc.vector.quantize_mx(out=pair[0][:, cols].bitcast(FP8X4), scales=pair[1][:, cols], in_=src)
 
+        w1_bf = {}
         w1_q = {}
-        w1_bf = []
-        for b in range(PASSES):
-            w1_bf.append(keep.tile([P, PACK, P, PACK], BF16, name="w1_bf%d" % b, align_bytes=64))
+
+        def deal_w1(s0, count):
+            b, t = divmod(s0, PACK)
+            w1_bf[s0] = keep.tile([P, count, P, PACK], BF16, name="w1_bf%d" % s0, align_bytes=64)
+            nc.scalar.copy(w1_bf[s0][:], w1_raw[b][:].rearrange("p j (m t) -> p t m j", t=PACK)[:, t : t + count, :, :])
+
+        def quantize_w1(s0, count, tag):
+            pair = mx_tiles("w1q%d" % s0, count * P, tag)
+            quantize(pair, slice(0, count * P), w1_bf[s0][:].rearrange("p t m j -> p (t m j)"))
+            for i in range(count):
+                w1_q[s0 + i] = (pair[0][:, i * P : (i + 1) * P], pair[1][:, i * P : (i + 1) * P])
 
         h = {}
         th = {}
         lin = {}
-        off_th = {}
         off_lin = {}
         off_term = {}
-
-        def on_vector(s):
-            return CHUNKS if s < 2 else 1
+        DIRECT = 2
 
         def stage1(s):
             b, t = divmod(s, PACK)
             cols = slice(s * P, (s + 1) * P)
-            w1_words, w1_planes = w1_q[b]
-            nv = on_vector(s)
-            if nv < CHUNKS:
-                off_th[s] = ring.tile([P, (CHUNKS - nv) * BANK], F32, name="off_th", bufs=1)
-                off_lin[s] = ring.tile([P, (CHUNKS - nv) * BANK], F32, name="off_lin")
-                off_term[s] = ring.tile([P, (CHUNKS - nv) * BANK], F32, name="off_term")
+            if s >= DIRECT:
+                off_th = ring.tile([P, S], F32, name="off_th", bufs=1)
+                off_lin[s] = ring.tile([P, S], F32, name="off_lin")
+                off_term[s] = ring.tile([P, S], F32, name="off_term")
             for c in range(CHUNKS):
                 toks = slice(c * BANK, (c + 1) * BANK)
                 arg = psum.tile([P, BANK], F32, name="arg", tag="bank%d" % (2 * c))
@@ -146,33 +145,29 @@ def tile_list_laundering_alert_scores_kernel(
                 )
                 lin[s, c] = psum.tile([P, BANK], F32, name="lin", tag="bank%d" % (2 * c + 1))
                 nc.tensor.matmul_mx(
-                    out=lin[s, c][:], lhsT=w1_words[:, t * P : (t + 1) * P].bitcast(FP8X4),
-                    lhsT_scale=w1_planes[:, t * P : (t + 1) * P],
+                    out=lin[s, c][:], lhsT=w1_q[s][0].bitcast(FP8X4), lhsT_scale=w1_q[s][1],
                     rhs=v_w[:, toks].bitcast(FP8X4), rhs_scale=v_b[:, toks], start=True, stop=True,
                 )
-                if c < nv:
-                    th[s, c] = ring.tile([P, BANK], F32, name="th", bufs=4)
+                if s < DIRECT:
+                    th[s, c] = ring.tile([P, BANK], F32, name="th", tag="quarter", bufs=4)
                     nc.scalar.activation(th[s, c][:], arg[:], ACT.Tanh)
                 else:
-                    part = slice((c - nv) * BANK, (c - nv + 1) * BANK)
-                    nc.scalar.activation(off_th[s][:, part], arg[:], ACT.Tanh)
-                    nc.scalar.copy(off_lin[s][:, part], lin[s, c][:])
-            if nv < CHUNKS:
-                nc.scalar.activation(off_term[s][:], off_th[s][:], ACT.Copy, scale=gain_sb[:, b, t : t + 1])
-
-        def open_h(s):
-            h[s] = ring.tile([P, S], F32, name="h")
-            nv = on_vector(s)
-            if nv < CHUNKS:
-                nc.gpsimd.tensor_tensor(h[s][:, nv * BANK :], off_lin[s][:], off_term[s][:], ALU.add)
+                    nc.scalar.activation(off_th[:, toks], arg[:], ACT.Tanh)
+                    nc.scalar.copy(off_lin[s][:, toks], lin[s, c][:])
+            if s >= DIRECT:
+                nc.scalar.activation(off_term[s][:], off_th[:], ACT.Copy, scale=gain_sb[:, b, t : t + 1])
 
         def combine(s):
             b, t = divmod(s, PACK)
-            for c in range(on_vector(s)):
-                nc.vector.scalar_tensor_tensor(
-                    out=h[s][:, c * BANK : (c + 1) * BANK], in0=th[s, c][:], scalar=gain_sb[:, b, t : t + 1],
-                    in1=lin[s, c][:], op0=ALU.mult, op1=ALU.add,
-                )
+            h[s] = keep.tile([P, S], F32, name="h", tag="window%d" % (s % 4))
+            if s >= DIRECT:
+                nc.gpsimd.tensor_tensor(h[s][:], off_lin[s][:], off_term[s][:], ALU.add)
+            else:
+                for c in range(CHUNKS):
+                    nc.vector.scalar_tensor_tensor(
+                        out=h[s][:, c * BANK : (c + 1) * BANK], in0=th[s, c][:], scalar=gain_sb[:, b, t : t + 1],
+                        in1=lin[s, c][:], op0=ALU.mult, op1=ALU.add,
+                    )
 
         w3_q = {}
         a2_q = {}
@@ -193,76 +188,75 @@ def tile_list_laundering_alert_scores_kernel(
                 rhs=a2_q[a][0][:].bitcast(FP8X4), rhs_scale=a2_q[a][1][:], start=(a == 0), stop=(a == PASSES - 1),
             )
 
-        def flat(tile4):
-            return tile4[:].rearrange("p t m j -> p (t m j)")
-
-        def flat3(tile3):
+        def flat(tile3):
             return tile3[:].rearrange("p c t -> p (c t)")
 
-        deal_w1(w1_bf[0], 0, 0, PACK)
-        w1_q[0] = quantize(flat(w1_bf[0]), "w1a", "w1a_w")
+        deal_w1(0, 4)
+        quantize_w1(0, 4, "w1q0_w")
         for c in range(CHUNKS):
             gather_words(c)
         stage1(0)
-        open_h(0)
         combine(0)
-        deal_w1(w1_bf[1], 1, 0, PACK)
+        deal_w1(4, 2)
         stage1(1)
-        open_h(1)
 
         a2_f32 = {}
-        a2_bf = {}
-        w3_bf = {}
-        HALF = PAIRS // 2
-        QUART = KEPT // 2
+        HALF = KEPT // 2
+        halves = [slice(0, HALF), slice(HALF, KEPT)]
         for s in range(SLICES):
             a, t = divmod(s, PACK)
-            last = s == SLICES - 1
-            if not last:
-                combine(s + 1)
-            if s in (1, 2):
-                w3_bf[s - 1] = ring.tile([P, N, PACK], BF16, name="w3_bf", align_bytes=64)
-                interleave(nc.scalar.copy, w3_bf[s - 1][:], w3_raw[s - 1][:])
-            if s == PACK:
-                a2_bf[0] = ring.tile([P, KEPT, PACK], BF16, name="a2_bf", align_bytes=64)
-                interleave(nc.scalar.copy, a2_bf[0][:], a2_f32[0][:])
+            if s == 1:
+                deal_w1(6, 2)
             if s + 2 < SLICES:
                 stage1(s + 2)
-            g1 = keep.tile([P, PAIRS], F32, name="g1", tag="g1_%d" % s if s in (1, 3, 4, 7) else "g1", align_bytes=64)
-            nc.vector.tensor_copy(g1[:], h[s][:].indirect(p1[:]))
-            g2 = ring.tile([P, PAIRS], F32, name="g2")
-            for u in range(2):
-                nc.vector.tensor_copy(g2[:, u * HALF : (u + 1) * HALF], h[s][:].indirect(p2[:, u * 32 : (u + 1) * 32]))
-            a1 = ring.tile([P, PAIRS], F32, name="a1")
-            for u in range(2):
-                part = slice(u * HALF, (u + 1) * HALF)
-                nc.vector.tensor_tensor(a1[:, part], g1[:, part], g2[:, part], ALU.max)
-            if s == 1:
-                w1_q[1] = quantize(flat(w1_bf[1]), "w1b", "g1_%d" % s)
-            if s in (3, 4):
-                w3_q[s - 3] = quantize(flat3(w3_bf[s - 3]), "w3_%d" % (s - 3), "g1_%d" % s)
-            if last:
-                a2_q[0] = quantize(flat3(a2_bf[0]), "a2_0", "g1_%d" % s)
+            if s == SLICES - 2:
+                for a3 in range(PASSES):
+                    w3_raw = keep.tile([P, PACK, N], F32, name="w3_raw", tag="raw%d" % a3)
+                    nc.sync.dma_start(w3_raw[:], w3[512 * a3 : 512 * (a3 + 1), :].rearrange("(p j) c -> p j c", j=PACK))
+                    w3_bf = ring.tile([P, N, PACK], BF16, name="w3_bf", align_bytes=64)
+                    interleave(nc.scalar.copy, w3_bf[:], w3_raw[:])
+                    w3_q[a3] = mx_tiles("w3q%d" % a3, N, "w3q%d" % a3)
+                    quantize(w3_q[a3], slice(0, N), flat(w3_bf))
+                a2_bf = keep.tile([P, KEPT, PACK], BF16, name="a2_bf", align_bytes=64)
+                interleave(nc.scalar.copy, a2_bf[:], a2_f32[0][:])
+                a2_q[0] = mx_tiles("a2q0", KEPT, "a2q0")
+                quantize(a2_q[0], slice(0, KEPT), flat(a2_bf))
                 for o in range(OUT_TILES):
                     stage2(0, o)
-            g3 = ring.tile([P, KEPT], F32, name="g3")
-            for u in range(2):
-                nc.vector.tensor_copy(g3[:, u * QUART : (u + 1) * QUART], a1[:].indirect(p3[:, u * 16 : (u + 1) * 16]))
+            g1_tag = "g1_%d" % s if s in (1, 3) else "g1"
+            g1 = keep.tile([P, PAIRS], F32, name="g1", tag=g1_tag, align_bytes=64)
+            nc.vector.tensor_copy(g1[:], h[s][:].indirect(p1[:]))
+            g2 = keep.tile([P, PAIRS], F32, name="g2")
+            nc.vector.tensor_copy(g2[:], h[s][:].indirect(p2[:]))
+            g4 = keep.tile([P, KEPT], F32, name="g4")
+            nc.vector.tensor_copy(g4[:, halves[0]], h[s][:].indirect(p4[:, 0:16]))
+            a1 = keep.tile([P, PAIRS], F32, name="a1", tag="window%d" % ((s + 2) % 4))
+            nc.vector.tensor_tensor(a1[:], g1[:], g2[:], ALU.max)
+            if s in (1, 3):
+                quantize_w1(s + 3, 2, g1_tag)
+            nc.vector.tensor_copy(g4[:, halves[1]], h[s][:].indirect(p4[:, 16:32]))
             if t == 0:
                 a2_f32[a] = ring.tile([P, PACK, KEPT], F32, name="a2_f32")
             for u in range(2):
-                part = slice(u * QUART, (u + 1) * QUART)
-                nc.vector.tensor_tensor(a2_f32[a][:, t, part], h[s][:].indirect(p4[:, u * 16 : (u + 1) * 16]), g3[:, part], ALU.mult)
+                nc.vector.tensor_tensor(
+                    a2_f32[a][:, t, halves[u]], a1[:].indirect(p3[:, u * 16 : (u + 1) * 16]), g4[:, halves[u]], ALU.mult
+                )
+            if s == 0:
+                combine(1)
             if s + 2 < SLICES:
-                open_h(s + 2)
+                combine(s + 2)
 
-        a2_bf[1] = ring.tile([P, KEPT, PACK], BF16, name="a2_bf", align_bytes=64)
-        interleave(nc.vector.tensor_copy, a2_bf[1][:], a2_f32[1][:])
-        a2_q[1] = quantize(flat3(a2_bf[1]), "a2_1", "a2_1_w")
+        a2_q[1] = mx_tiles("a2q1", KEPT, "a2q1")
+        last_bf = []
+        for u, engine_copy in enumerate((nc.scalar.copy, nc.vector.tensor_copy)):
+            last_bf.append(ring.tile([P, HALF, PACK], BF16, name="last_bf", align_bytes=64))
+            interleave(engine_copy, last_bf[u][:], a2_f32[1][:, :, halves[u]])
+        for u in range(2):
+            quantize(a2_q[1], halves[u], flat(last_bf[u]))
         for o in range(OUT_TILES):
             stage2(1, o)
             tb = ring.tile([P, KEPT], F32, name="tb")
             nc.scalar.activation(tb[:], bounded[o][:], ACT.Tanh)
-            res = ring.tile([P, KEPT], F32, name="res", bufs=4)
+            res = ring.tile([P, KEPT], F32, name="res", tag="quarter", bufs=4)
             nc.vector.tensor_tensor(res[:], plain[o][:], tb[:], ALU.max)
             nc.sync.dma_start(out[o * P : (o + 1) * P, :], res[:])

@@ -171,21 +171,24 @@ def tile_list_laundering_alert_scores_kernel(
 
         w3_q = {}
         a2_q = {}
-        bounded = {}
-        plain = {}
+        scores = {}
+        HALF = KEPT // 2
+        halves = [slice(0, HALF), slice(HALF, KEPT)]
 
-        def stage2(a, o):
+        def stage2(a, u, o):
             cols = slice(o * P, (o + 1) * P)
             if a == 0:
-                bounded[o] = psum.tile([P, KEPT], F32, name="bounded", tag="bank%d" % (2 * o))
-                plain[o] = psum.tile([P, KEPT], F32, name="plain", tag="bank%d" % (2 * o + 1))
+                scores[u, o] = psum.tile([P, 2, HALF], F32, name="scores", tag="bank%d" % (OUT_TILES * u + o))
             nc.tensor.matmul_mx(
-                out=bounded[o][:], lhsT=w3_q[a][0][:, cols].bitcast(FP8X4), lhsT_scale=w3_q[a][1][:, cols],
-                rhs=a2_q[a][0][:].bitcast(FP8X4), rhs_scale=a2_q[a][1][:], start=(a == 0), stop=(a == PASSES - 1),
+                out=scores[u, o][:, 0, :], lhsT=w3_q[a][0][:, cols].bitcast(FP8X4), lhsT_scale=w3_q[a][1][:, cols],
+                rhs=a2_q[a][0][:, halves[u]].bitcast(FP8X4), rhs_scale=a2_q[a][1][:, halves[u]],
+                start=(a == 0), stop=False,
             )
             nc.tensor.matmul_mx(
-                out=plain[o][:], lhsT=w4_w[:, a, cols].bitcast(FP8X4), lhsT_scale=w4_b[:, a * N + o * P : a * N + (o + 1) * P],
-                rhs=a2_q[a][0][:].bitcast(FP8X4), rhs_scale=a2_q[a][1][:], start=(a == 0), stop=(a == PASSES - 1),
+                out=scores[u, o][:, 1, :], lhsT=w4_w[:, a, cols].bitcast(FP8X4),
+                lhsT_scale=w4_b[:, a * N + o * P : a * N + (o + 1) * P],
+                rhs=a2_q[a][0][:, halves[u]].bitcast(FP8X4), rhs_scale=a2_q[a][1][:, halves[u]],
+                start=False, stop=(a == PASSES - 1),
             )
 
         def flat(tile3):
@@ -197,15 +200,14 @@ def tile_list_laundering_alert_scores_kernel(
             gather_words(c)
         stage1(0)
         combine(0)
-        deal_w1(4, 2)
         stage1(1)
+        combine(1)
+        deal_w1(4, 2)
 
         a2_f32 = {}
-        HALF = KEPT // 2
-        halves = [slice(0, HALF), slice(HALF, KEPT)]
         for s in range(SLICES):
             a, t = divmod(s, PACK)
-            if s == 1:
+            if s == 2:
                 deal_w1(6, 2)
             if s + 2 < SLICES:
                 stage1(s + 2)
@@ -221,8 +223,9 @@ def tile_list_laundering_alert_scores_kernel(
                 interleave(nc.scalar.copy, a2_bf[:], a2_f32[0][:])
                 a2_q[0] = mx_tiles("a2q0", KEPT, "a2q0")
                 quantize(a2_q[0], slice(0, KEPT), flat(a2_bf))
-                for o in range(OUT_TILES):
-                    stage2(0, o)
+                for u in range(2):
+                    for o in range(OUT_TILES):
+                        stage2(0, u, o)
             g1_tag = "g1_%d" % s if s in (1, 3) else "g1"
             g1 = keep.tile([P, PAIRS], F32, name="g1", tag=g1_tag, align_bytes=64)
             nc.vector.tensor_copy(g1[:], h[s][:].indirect(p1[:]))
@@ -234,29 +237,34 @@ def tile_list_laundering_alert_scores_kernel(
             nc.vector.tensor_tensor(a1[:], g1[:], g2[:], ALU.max)
             if s in (1, 3):
                 quantize_w1(s + 3, 2, g1_tag)
-            nc.vector.tensor_copy(g4[:, halves[1]], h[s][:].indirect(p4[:, 16:32]))
             if t == 0:
                 a2_f32[a] = ring.tile([P, PACK, KEPT], F32, name="a2_f32")
-            for u in range(2):
+
+            def product(u):
                 nc.vector.tensor_tensor(
                     a2_f32[a][:, t, halves[u]], a1[:].indirect(p3[:, u * 16 : (u + 1) * 16]), g4[:, halves[u]], ALU.mult
                 )
-            if s == 0:
-                combine(1)
+
+            if s == SLICES - 1:
+                product(0)
+            nc.vector.tensor_copy(g4[:, halves[1]], h[s][:].indirect(p4[:, 16:32]))
+            if s < SLICES - 1:
+                product(0)
+            product(1)
             if s + 2 < SLICES:
                 combine(s + 2)
 
         a2_q[1] = mx_tiles("a2q1", KEPT, "a2q1")
-        last_bf = []
         for u, engine_copy in enumerate((nc.scalar.copy, nc.vector.tensor_copy)):
-            last_bf.append(ring.tile([P, HALF, PACK], BF16, name="last_bf", align_bytes=64))
-            interleave(engine_copy, last_bf[u][:], a2_f32[1][:, :, halves[u]])
+            last_bf = ring.tile([P, HALF, PACK], BF16, name="last_bf", align_bytes=64)
+            interleave(engine_copy, last_bf[:], a2_f32[1][:, :, halves[u]])
+            quantize(a2_q[1], halves[u], flat(last_bf))
+            for o in range(OUT_TILES):
+                stage2(1, u, o)
         for u in range(2):
-            quantize(a2_q[1], halves[u], flat(last_bf[u]))
-        for o in range(OUT_TILES):
-            stage2(1, o)
-            tb = ring.tile([P, KEPT], F32, name="tb")
-            nc.scalar.activation(tb[:], bounded[o][:], ACT.Tanh)
-            res = ring.tile([P, KEPT], F32, name="res", tag="quarter", bufs=4)
-            nc.vector.tensor_tensor(res[:], plain[o][:], tb[:], ALU.max)
-            nc.sync.dma_start(out[o * P : (o + 1) * P, :], res[:])
+            for o in range(OUT_TILES):
+                tb = ring.tile([P, HALF], F32, name="tb", bufs=4)
+                nc.scalar.activation(tb[:], scores[u, o][:, 0, :], ACT.Tanh)
+                res = ring.tile([P, HALF], F32, name="res", bufs=8)
+                nc.vector.tensor_tensor(res[:], scores[u, o][:, 1, :], tb[:], ALU.max)
+                nc.sync.dma_start(out[o * P : (o + 1) * P, halves[u]], res[:])

@@ -18,11 +18,20 @@ ACT = mybir.ActivationFunctionType
 
 P = 128
 PACK = 4
+PASS_ROWS = P * PACK
 BANK = 512
 CHUNKS = S // BANK
 SLICES = H // P
-PASSES = H // (P * PACK)
+PASSES = H // PASS_ROWS
 OUT_TILES = N // P
+QUADRANTS = 4
+PER_COLUMN = 16
+HALF = KEPT // 2
+HEAD = 2
+WINDOWS = 4
+SPACER = 128
+SCALE_GATHERS = 2
+TABLE_PIECE_BYTES = 4096
 
 
 def tile_list_laundering_alert_scores_kernel(
@@ -35,9 +44,12 @@ def tile_list_laundering_alert_scores_kernel(
         psum = ctx.enter_context(tc.psum_pool(name="psum", bufs=1))
 
         def load_list(source, name):
-            t = keep.tile(list(source.shape), U16, name=name)
-            nc.sync.dma_start(t[:], source)
-            return t
+            offsets = keep.tile(list(source.shape), U16, name=name)
+            nc.sync.dma_start(offsets[:], source)
+            return offsets
+
+        def entries(first, last):
+            return slice(first // PER_COLUMN, last // PER_COLUMN)
 
         tab_b = keep.tile([P, T], U8, tag="scales_then_words", align_bytes=64)
         nc.vector.memset(tab_b[:].bitcast(I32), 0)
@@ -47,135 +59,143 @@ def tile_list_laundering_alert_scores_kernel(
         nc.gpsimd.memset(w4_b[:].bitcast(I32), 0)
 
         idx = load_list(offs, "idx")
-        for q in range(4):
+        for q in range(QUADRANTS):
             nc.scalar.dma_start(tab_b[32 * q : 32 * q + 4, :].bitcast(I32), tab_scales[0, 4 * q : 4 * q + 4, :].bitcast(I32))
         p1 = load_list(pos1, "p1")
         p2 = load_list(pos2, "p2")
         p3 = load_list(pos3, "p3")
-        w1_raw = []
-        for b in range(PASSES):
-            w1_raw.append(keep.tile([P, PACK, BANK], F32, name="w1_raw%d" % b, tag="raw%d" % b))
+        w1_raw = [keep.tile([P, PACK, PASS_ROWS], F32, name="w1_raw%d" % a, tag="raw%d" % a) for a in range(PASSES)]
         w1_rows = w1.rearrange("(p j) c -> p j c", j=PACK)
         w2_w_raw = keep.tile([P, H // 2], I32, align_bytes=64)
-        nc.sync.dma_start(w1_raw[0][:], w1_rows[:, :, 0:BANK])
+        nc.sync.dma_start(w1_raw[0][:], w1_rows[:, :, 0:PASS_ROWS])
         nc.sync.dma_start(w2_w_raw[:], w2_words[0].bitcast(I32))
-        tab_w = keep.tile([P, T], I32, align_bytes=64)
-        nc.sync.dma_start(tab_w[:], tab_words[0].rearrange("p t i -> p (t i)").bitcast(I32), max_dma_last_dim=4096)
-        for q in range(4):
+        tab_w = keep.tile([P, T], I32, tag="table_words", align_bytes=64)
+        nc.sync.dma_start(
+            tab_w[:], tab_words[0].rearrange("p t i -> p (t i)").bitcast(I32), max_dma_last_dim=TABLE_PIECE_BYTES
+        )
+        for q in range(QUADRANTS):
             nc.scalar.dma_start(w2_b_raw[32 * q : 32 * q + 4, :].bitcast(I32), w2_scales[0, 4 * q : 4 * q + 4, :].bitcast(I32))
         gain_sb = keep.tile([P, PASSES, PACK], F32)
-        nc.sync.dma_start(gain_sb[:], gain.rearrange("(b p t) -> p b t", p=P, t=PACK))
+        nc.sync.dma_start(gain_sb[:], gain.rearrange("(a p t) -> p a t", p=P, t=PACK))
         p4 = load_list(pos4, "p4")
-        nc.sync.dma_start(w1_raw[1][:], w1_rows[:, :, BANK : 2 * BANK])
+        nc.sync.dma_start(w1_raw[1][:], w1_rows[:, :, PASS_ROWS : 2 * PASS_ROWS])
         w4_w = keep.tile([P, PASSES, N], I32, align_bytes=64)
         nc.sync.dma_start(w4_w[:], w4_words.rearrange("a p c i -> p a (c i)").bitcast(I32))
-        for q in range(4):
+        for q in range(QUADRANTS):
             nc.sync.dma_start(
                 w4_b[32 * q : 32 * q + 4, :].bitcast(I32).rearrange("r (a c) -> r a c", a=PASSES),
                 w4_scales[:, 4 * q : 4 * q + 4, :].bitcast(I32).rearrange("a r c -> r a c"),
             )
 
         v_b = keep.tile([P, S], U8, align_bytes=64)
-        for c in range(2):
-            nc.vector.tensor_copy(v_b[:, c * 1024 : (c + 1) * 1024], tab_b[:].indirect(idx[:, c * 64 : (c + 1) * 64]))
-
+        width = S // SCALE_GATHERS
+        for g in range(SCALE_GATHERS):
+            nc.vector.tensor_copy(
+                v_b[:, g * width : (g + 1) * width], tab_b[:].indirect(idx[:, entries(g * width, (g + 1) * width)])
+            )
         v_w = keep.tile([P, S], U32, tag="scales_then_words", align_bytes=64)
 
         def gather_words(c):
             nc.vector.tensor_copy(
-                v_w[:, c * BANK : (c + 1) * BANK], tab_w[:].bitcast(U32).indirect(idx[:, c * 32 : (c + 1) * 32])
+                v_w[:, c * BANK : (c + 1) * BANK], tab_w[:].bitcast(U32).indirect(idx[:, entries(c * BANK, (c + 1) * BANK)])
             )
 
         w2_w = keep.tile([P, 2 * H], U8, align_bytes=64)
-        nc.scalar.copy(
-            w2_w[:].bitcast(U16).rearrange("p (b t m) -> p b t m", b=PASSES, t=PACK),
-            w2_w_raw[:].bitcast(U16).rearrange("p (b m t) -> p b t m", b=PASSES, t=PACK),
-        )
-        w2_b = keep.tile([P, H], U8, align_bytes=64)
-        w2_b_dealt = w2_b[:].rearrange("p (b t m) -> p b t m", b=PASSES, t=PACK)
-        w2_b_given = w2_b_raw[:].rearrange("p (b m t) -> p b t m", b=PASSES, t=PACK)
-        for b, t0, t1 in ((0, 0, 1), (0, 1, PACK), (1, 0, PACK)):
-            nc.gpsimd.tensor_copy(w2_b_dealt[:, b, t0:t1, :], w2_b_given[:, b, t0:t1, :])
+        w2_w_dealt = w2_w[:].bitcast(U16).rearrange("p (a t m) -> p a t m", a=PASSES, t=PACK)
+        w2_w_given = w2_w_raw[:].bitcast(U16).rearrange("p (a m t) -> p a t m", a=PASSES, t=PACK)
+        w2_b_given = w2_b_raw[:].rearrange("p (a m t) -> p a t m", a=PASSES, t=PACK)
+        w2_b = {}
+        w1_bf = {}
+        w1_q = {}
+
+        def deal_w2_words(s0, count):
+            a, t = divmod(s0, PACK)
+            nc.scalar.copy(w2_w_dealt[:, a, t : t + count, :], w2_w_given[:, a, t : t + count, :])
+
+        def deal_w2_scales(s0, count, tag):
+            a, t = divmod(s0, PACK)
+            dealt = keep.tile([P, count * P], U8, name="w2_b%d" % s0, tag=tag, align_bytes=64)
+            nc.gpsimd.tensor_copy(dealt[:].rearrange("p (t m) -> p t m", t=count), w2_b_given[:, a, t : t + count, :])
+            for i in range(count):
+                w2_b[s0 + i] = dealt[:, i * P : (i + 1) * P]
+
+        def deal_w1(s0, count, tag):
+            a, t = divmod(s0, PACK)
+            w1_bf[s0] = keep.tile([P, count, P, PACK], BF16, name="w1_bf%d" % s0, tag=tag, align_bytes=64)
+            nc.scalar.copy(w1_bf[s0][:], w1_raw[a][:].rearrange("p j (m t) -> p t m j", t=PACK)[:, t : t + count, :, :])
+
+        def mx_tiles(name, columns, tag):
+            words = keep.tile([P, columns], U32, name=name + "_w", tag=tag, align_bytes=64)
+            scale_bytes = keep.tile([P, columns], U8, name=name + "_b", align_bytes=64)
+            return words, scale_bytes
+
+        def quantize(operand, cols, src):
+            nc.vector.quantize_mx(out=operand[0][:, cols].bitcast(FP8X4), scales=operand[1][:, cols], in_=src)
+
+        def quantize_w1(s0, count, tag):
+            operand = mx_tiles("w1q%d" % s0, count * P, tag)
+            quantize(operand, slice(0, count * P), w1_bf[s0][:].rearrange("p t m j -> p (t m j)"))
+            for i in range(count):
+                w1_q[s0 + i] = (operand[0][:, i * P : (i + 1) * P], operand[1][:, i * P : (i + 1) * P])
 
         def interleave(engine_copy, dst, src):
             engine_copy(dst.rearrange("p (c i) t -> p c t i", i=4), src.rearrange("p t (c i) -> p c t i", i=4))
 
-        def mx_tiles(name, width, tag):
-            words = keep.tile([P, width], U32, name=name + "_w", tag=tag, align_bytes=64)
-            planes = keep.tile([P, width], U8, name=name + "_b", align_bytes=64)
-            return words, planes
-
-        def quantize(pair, cols, src):
-            nc.vector.quantize_mx(out=pair[0][:, cols].bitcast(FP8X4), scales=pair[1][:, cols], in_=src)
-
-        w1_bf = {}
-        w1_q = {}
-
-        def deal_w1(s0, count):
-            b, t = divmod(s0, PACK)
-            w1_bf[s0] = keep.tile([P, count, P, PACK], BF16, name="w1_bf%d" % s0, align_bytes=64)
-            nc.scalar.copy(w1_bf[s0][:], w1_raw[b][:].rearrange("p j (m t) -> p t m j", t=PACK)[:, t : t + count, :, :])
-
-        def quantize_w1(s0, count, tag):
-            pair = mx_tiles("w1q%d" % s0, count * P, tag)
-            quantize(pair, slice(0, count * P), w1_bf[s0][:].rearrange("p t m j -> p (t m j)"))
-            for i in range(count):
-                w1_q[s0 + i] = (pair[0][:, i * P : (i + 1) * P], pair[1][:, i * P : (i + 1) * P])
-
         h = {}
-        th = {}
-        lin = {}
-        off_lin = {}
-        off_term = {}
-        DIRECT = 2
+        linear_sb = {}
+        gained_sb = {}
 
-        def stage1(s):
-            b, t = divmod(s, PACK)
-            cols = slice(s * P, (s + 1) * P)
-            if s >= DIRECT:
-                off_th = ring.tile([P, S], F32, name="off_th", bufs=1)
-                off_lin[s] = ring.tile([P, S], F32, name="off_lin")
-                off_term[s] = ring.tile([P, S], F32, name="off_term")
+        def first_products(s, c, arg_bank, linear_bank):
+            toks = slice(c * BANK, (c + 1) * BANK)
+            arg = psum.tile([P, BANK], F32, name="arg", tag="bank%d" % arg_bank)
+            nc.tensor.matmul_mx(
+                out=arg[:], lhsT=w2_w[:, 2 * s * P : 2 * (s + 1) * P].bitcast(FP4X4), lhsT_scale=w2_b[s],
+                rhs=v_w[:, toks].bitcast(FP8X4), rhs_scale=v_b[:, toks], start=True, stop=True,
+            )
+            linear = psum.tile([P, BANK], F32, name="linear", tag="bank%d" % linear_bank)
+            nc.tensor.matmul_mx(
+                out=linear[:], lhsT=w1_q[s][0].bitcast(FP8X4), lhsT_scale=w1_q[s][1],
+                rhs=v_w[:, toks].bitcast(FP8X4), rhs_scale=v_b[:, toks], start=True, stop=True,
+            )
+            return arg, linear
+
+        def gain_column(s):
+            a, t = divmod(s, PACK)
+            return gain_sb[:, a, t : t + 1]
+
+        def head_chunk(s, c):
+            arg, linear = first_products(s, c, s, 2 + 2 * ((c + 2) % 3) + s)
+            if (s, c) == (HEAD - 1, CHUNKS - 1):
+                th = keep.tile([P, BANK], F32, name="th_last", tag="pair_0", align_bytes=64)
+            else:
+                th = ring.tile([P, BANK], F32, name="th", tag="quarter", bufs=HEAD * CHUNKS)
+            nc.scalar.activation(th[:], arg[:], ACT.Tanh)
+            nc.vector.scalar_tensor_tensor(
+                out=h[s][:, c * BANK : (c + 1) * BANK], in0=th[:], scalar=gain_column(s), in1=linear[:],
+                op0=ALU.mult, op1=ALU.add,
+            )
+
+        def first_stage_terms(s):
+            tanh_sb = keep.tile([P, S], F32, name="tanh_sb", tag="tanh_first" if s == HEAD else "tanh_later", align_bytes=64)
+            linear_sb[s] = ring.tile([P, S], F32, name="linear_sb")
+            gained_sb[s] = ring.tile([P, S], F32, name="gained_sb")
             for c in range(CHUNKS):
                 toks = slice(c * BANK, (c + 1) * BANK)
-                arg = psum.tile([P, BANK], F32, name="arg", tag="bank%d" % (2 * c))
-                nc.tensor.matmul_mx(
-                    out=arg[:], lhsT=w2_w[:, 2 * s * P : 2 * (s + 1) * P].bitcast(FP4X4), lhsT_scale=w2_b[:, cols],
-                    rhs=v_w[:, toks].bitcast(FP8X4), rhs_scale=v_b[:, toks], start=True, stop=True,
-                )
-                lin[s, c] = psum.tile([P, BANK], F32, name="lin", tag="bank%d" % (2 * c + 1))
-                nc.tensor.matmul_mx(
-                    out=lin[s, c][:], lhsT=w1_q[s][0].bitcast(FP8X4), lhsT_scale=w1_q[s][1],
-                    rhs=v_w[:, toks].bitcast(FP8X4), rhs_scale=v_b[:, toks], start=True, stop=True,
-                )
-                if s < DIRECT:
-                    th[s, c] = ring.tile([P, BANK], F32, name="th", tag="quarter", bufs=4)
-                    nc.scalar.activation(th[s, c][:], arg[:], ACT.Tanh)
-                else:
-                    nc.scalar.activation(off_th[:, toks], arg[:], ACT.Tanh)
-                    nc.scalar.copy(off_lin[s][:, toks], lin[s, c][:])
-            if s >= DIRECT:
-                nc.scalar.activation(off_term[s][:], off_th[:], ACT.Copy, scale=gain_sb[:, b, t : t + 1])
+                arg, linear = first_products(s, c, 2 * c, 2 * c + 1)
+                nc.scalar.activation(tanh_sb[:, toks], arg[:], ACT.Tanh)
+                nc.scalar.copy(linear_sb[s][:, toks], linear[:])
+            nc.scalar.activation(gained_sb[s][:], tanh_sb[:], ACT.Copy, scale=gain_column(s))
 
-        def combine(s):
-            b, t = divmod(s, PACK)
-            h[s] = keep.tile([P, S], F32, name="h", tag="window%d" % (s % 4))
-            if s >= DIRECT:
-                nc.gpsimd.tensor_tensor(h[s][:], off_lin[s][:], off_term[s][:], ALU.add)
-            else:
-                for c in range(CHUNKS):
-                    nc.vector.scalar_tensor_tensor(
-                        out=h[s][:, c * BANK : (c + 1) * BANK], in0=th[s, c][:], scalar=gain_sb[:, b, t : t + 1],
-                        in1=lin[s, c][:], op0=ALU.mult, op1=ALU.add,
-                    )
+        def add_terms(s):
+            h[s] = keep.tile([P, S], F32, name="h", tag="window%d" % (s % WINDOWS))
+            nc.gpsimd.tensor_tensor(h[s][:], linear_sb[s][:], gained_sb[s][:], ALU.add)
 
         w3_q = {}
         a2_q = {}
         scores = {}
-        HALF = KEPT // 2
         halves = [slice(0, HALF), slice(HALF, KEPT)]
 
-        def stage2(a, u, o):
+        def second_products(a, u, o):
             cols = slice(o * P, (o + 1) * P)
             if a == 0:
                 scores[u, o] = psum.tile([P, 2, HALF], F32, name="scores", tag="bank%d" % (OUT_TILES * u + o))
@@ -191,80 +211,93 @@ def tile_list_laundering_alert_scores_kernel(
                 start=False, stop=(a == PASSES - 1),
             )
 
-        def flat(tile3):
-            return tile3[:].rearrange("p c t -> p (c t)")
-
-        deal_w1(0, 4)
-        quantize_w1(0, 4, "w1q0_w")
+        for s0 in (0, HEAD):
+            deal_w1(s0, HEAD, "w1_bf%d" % s0)
+            deal_w2_words(s0, HEAD)
+            deal_w2_scales(s0, HEAD, "w2_b%d" % s0)
+            quantize_w1(s0, HEAD, "w1q%d" % s0)
+        deal_w2_words(PACK, PACK)
         for c in range(CHUNKS):
             gather_words(c)
-        stage1(0)
-        combine(0)
-        stage1(1)
-        combine(1)
-        deal_w1(4, 2)
+        deal_w2_scales(PACK, PACK, "table_words")
+        for s in range(HEAD):
+            h[s] = keep.tile([P, S], F32, name="h", tag="window%d" % s)
+        for c in range(CHUNKS):
+            for s in range(HEAD):
+                head_chunk(s, c)
+        deal_w1(PACK, 1, "w1q0")
 
         a2_f32 = {}
+        last = SLICES - 1
         for s in range(SLICES):
             a, t = divmod(s, PACK)
-            if s == 2:
-                deal_w1(6, 2)
+            if s == 1:
+                deal_w1(PACK + 1, PACK - 1, "tanh_first")
             if s + 2 < SLICES:
-                stage1(s + 2)
-            if s == SLICES - 2:
+                first_stage_terms(s + 2)
+            if s == last - 1:
+                late_bf = keep.tile([P, (PASSES + 1) * N * PACK], BF16, name="late_bf", tag="tanh_later", align_bytes=64)
+                w3_bf = [late_bf[:, i * N * PACK : (i + 1) * N * PACK] for i in range(PASSES)]
+                a2_first_bf = late_bf[:, PASSES * N * PACK :]
+                interleave(nc.scalar.copy, a2_first_bf.rearrange("p (c t) -> p c t", t=PACK), a2_f32[0][:])
                 for a3 in range(PASSES):
                     w3_raw = keep.tile([P, PACK, N], F32, name="w3_raw", tag="raw%d" % a3)
-                    nc.sync.dma_start(w3_raw[:], w3[512 * a3 : 512 * (a3 + 1), :].rearrange("(p j) c -> p j c", j=PACK))
-                    w3_bf = ring.tile([P, N, PACK], BF16, name="w3_bf", align_bytes=64)
-                    interleave(nc.scalar.copy, w3_bf[:], w3_raw[:])
+                    nc.sync.dma_start(
+                        w3_raw[:], w3[PASS_ROWS * a3 : PASS_ROWS * (a3 + 1), :].rearrange("(p j) c -> p j c", j=PACK)
+                    )
+                    interleave(nc.scalar.copy, w3_bf[a3].rearrange("p (c t) -> p c t", t=PACK), w3_raw[:])
                     w3_q[a3] = mx_tiles("w3q%d" % a3, N, "w3q%d" % a3)
-                    quantize(w3_q[a3], slice(0, N), flat(w3_bf))
-                a2_bf = keep.tile([P, KEPT, PACK], BF16, name="a2_bf", align_bytes=64)
-                interleave(nc.scalar.copy, a2_bf[:], a2_f32[0][:])
-                a2_q[0] = mx_tiles("a2q0", KEPT, "a2q0")
-                quantize(a2_q[0], slice(0, KEPT), flat(a2_bf))
+                    quantize(w3_q[a3], slice(0, N), w3_bf[a3])
+
+            pair_tag = {1: "pair_1", 2: "pair_2", last: "pair_2"}.get(s, "pair_0")
+            pair = keep.tile([P, 2 * PAIRS], F32, name="pair", tag=pair_tag, align_bytes=64)
+            nc.vector.tensor_copy(pair[:, 0:PAIRS], h[s][:].indirect(p1[:]))
+            nc.vector.tensor_copy(pair[:, PAIRS:], h[s][:].indirect(p2[:]))
+            cut = HALF if s == last else KEPT - SPACER
+            parts = [slice(0, cut), slice(cut, KEPT)]
+            part_entries = [entries(0, cut), entries(cut, KEPT)]
+            deposit = keep.tile([P, KEPT], F32, name="deposit", tag="pair_1" if s == 0 else "deposit", align_bytes=64)
+            nc.vector.tensor_copy(deposit[:, parts[0]], h[s][:].indirect(p4[:, part_entries[0]]))
+            a1 = keep.tile([P, PAIRS], F32, name="a1", tag="window%d" % ((s + 2) % WINDOWS))
+            nc.vector.tensor_tensor(a1[:], pair[:, 0:PAIRS], pair[:, PAIRS:], ALU.max)
+            if s == 1:
+                quantize_w1(PACK, 1, pair_tag)
+            if s == 2:
+                quantize_w1(PACK + 1, PACK - 1, pair_tag)
+            if s == last:
+                a2_q[0] = mx_tiles("a2q0", KEPT, pair_tag)
+                quantize(a2_q[0], slice(0, KEPT), a2_first_bf)
                 for u in range(2):
                     for o in range(OUT_TILES):
-                        stage2(0, u, o)
-            g1_tag = "g1_%d" % s if s in (1, 3) else "g1"
-            g1 = keep.tile([P, PAIRS], F32, name="g1", tag=g1_tag, align_bytes=64)
-            nc.vector.tensor_copy(g1[:], h[s][:].indirect(p1[:]))
-            g2 = keep.tile([P, PAIRS], F32, name="g2")
-            nc.vector.tensor_copy(g2[:], h[s][:].indirect(p2[:]))
-            g4 = keep.tile([P, KEPT], F32, name="g4")
-            nc.vector.tensor_copy(g4[:, halves[0]], h[s][:].indirect(p4[:, 0:16]))
-            a1 = keep.tile([P, PAIRS], F32, name="a1", tag="window%d" % ((s + 2) % 4))
-            nc.vector.tensor_tensor(a1[:], g1[:], g2[:], ALU.max)
-            if s in (1, 3):
-                quantize_w1(s + 3, 2, g1_tag)
+                        second_products(0, u, o)
             if t == 0:
                 a2_f32[a] = ring.tile([P, PACK, KEPT], F32, name="a2_f32")
 
-            def product(u):
+            def product(part):
                 nc.vector.tensor_tensor(
-                    a2_f32[a][:, t, halves[u]], a1[:].indirect(p3[:, u * 16 : (u + 1) * 16]), g4[:, halves[u]], ALU.mult
+                    a2_f32[a][:, t, parts[part]], a1[:].indirect(p3[:, part_entries[part]]), deposit[:, parts[part]], ALU.mult
                 )
 
-            if s == SLICES - 1:
+            if s == last:
                 product(0)
-            nc.vector.tensor_copy(g4[:, halves[1]], h[s][:].indirect(p4[:, 16:32]))
-            if s < SLICES - 1:
+            nc.vector.tensor_copy(deposit[:, parts[1]], h[s][:].indirect(p4[:, part_entries[1]]))
+            if s < last:
                 product(0)
             product(1)
             if s + 2 < SLICES:
-                combine(s + 2)
+                add_terms(s + 2)
 
         a2_q[1] = mx_tiles("a2q1", KEPT, "a2q1")
         for u, engine_copy in enumerate((nc.scalar.copy, nc.vector.tensor_copy)):
-            last_bf = ring.tile([P, HALF, PACK], BF16, name="last_bf", align_bytes=64)
-            interleave(engine_copy, last_bf[:], a2_f32[1][:, :, halves[u]])
-            quantize(a2_q[1], halves[u], flat(last_bf))
+            a2_half_bf = ring.tile([P, HALF, PACK], BF16, name="a2_half_bf", align_bytes=64)
+            interleave(engine_copy, a2_half_bf[:], a2_f32[1][:, :, halves[u]])
+            quantize(a2_q[1], halves[u], a2_half_bf[:].rearrange("p c t -> p (c t)"))
             for o in range(OUT_TILES):
-                stage2(1, u, o)
+                second_products(1, u, o)
         for u in range(2):
             for o in range(OUT_TILES):
-                tb = ring.tile([P, HALF], F32, name="tb", bufs=4)
-                nc.scalar.activation(tb[:], scores[u, o][:, 0, :], ACT.Tanh)
-                res = ring.tile([P, HALF], F32, name="res", bufs=8)
-                nc.vector.tensor_tensor(res[:], scores[u, o][:, 1, :], tb[:], ALU.max)
-                nc.sync.dma_start(out[o * P : (o + 1) * P, halves[u]], res[:])
+                bounded = ring.tile([P, HALF], F32, name="bounded", bufs=OUT_TILES)
+                nc.scalar.activation(bounded[:], scores[u, o][:, 0, :], ACT.Tanh)
+                result = ring.tile([P, HALF], F32, name="result", tag="quarter", bufs=HEAD * CHUNKS)
+                nc.vector.tensor_tensor(result[:], scores[u, o][:, 1, :], bounded[:], ALU.max)
+                nc.sync.dma_start(out[o * P : (o + 1) * P, halves[u]], result[:])

from contextlib import ExitStack

import concourse.mybir as mybir

K, H, N, T, S, PAIRS, KEPT = 512, 1024, 512, 4096, 2048, 1024, 512
FLOPS = 2 * 2 * K * H * S + 2 * 2 * H * N * KEPT

F32 = mybir.dt.float32
BF16 = mybir.dt.bfloat16
I32 = mybir.dt.int32
U32 = mybir.dt.uint32
U16 = mybir.dt.uint16
U8 = mybir.dt.uint8
FP8X4 = mybir.dt.float8_e4m3fn_x4
FP4X4 = mybir.dt.float4_e2m1fn_x4
ALU = mybir.AluOpType
ACT = mybir.ActivationFunctionType

P = 128
PACK = 4
PASS_ROWS = P * PACK
BANK = 512
CHUNKS = S // BANK
SLICES = H // P
PASSES = H // PASS_ROWS
OUT_TILES = N // P
QUADRANTS = 4
PER_COLUMN = 16
HALF = KEPT // 2
HEAD = 2
WINDOWS = 4
SPACER = 128
SCALE_GATHERS = 2
TABLE_PIECE_BYTES = 4096


def tile_list_laundering_alert_scores_kernel(
    tc, tab_words, tab_scales, offs, pos1, pos2, pos3, pos4, w1, w2_words, w2_scales, gain, w3, w4_words, w4_scales, out
):
    nc = tc.nc
    with ExitStack() as ctx:
        keep = ctx.enter_context(tc.tile_pool(name="keep", bufs=1))
        ring = ctx.enter_context(tc.tile_pool(name="ring", bufs=2))
        psum = ctx.enter_context(tc.psum_pool(name="psum", bufs=1))

        def load_list(source, name):
            offsets = keep.tile(list(source.shape), U16, name=name)
            nc.sync.dma_start(offsets[:], source)
            return offsets

        def entries(first, last):
            return slice(first // PER_COLUMN, last // PER_COLUMN)

        tab_b = keep.tile([P, T], U8, tag="scales_then_words", align_bytes=64)
        nc.vector.memset(tab_b[:].bitcast(I32), 0)
        w2_b_raw = keep.tile([P, H], U8, align_bytes=64)
        nc.vector.memset(w2_b_raw[:].bitcast(I32), 0)
        w4_b = keep.tile([P, PASSES * N], U8, align_bytes=64)
        nc.gpsimd.memset(w4_b[:].bitcast(I32), 0)

        idx = load_list(offs, "idx")
        for q in range(QUADRANTS):
            nc.scalar.dma_start(tab_b[32 * q : 32 * q + 4, :].bitcast(I32), tab_scales[0, 4 * q : 4 * q + 4, :].bitcast(I32))
        p1 = load_list(pos1, "p1")
        p2 = load_list(pos2, "p2")
        p3 = load_list(pos3, "p3")
        w1_raw = [keep.tile([P, PACK, PASS_ROWS], F32, name="w1_raw%d" % a, tag="raw%d" % a) for a in range(PASSES)]
        w1_rows = w1.rearrange("(p j) c -> p j c", j=PACK)
        w2_w_raw = keep.tile([P, H // 2], I32, align_bytes=64)
        nc.sync.dma_start(w1_raw[0][:], w1_rows[:, :, 0:PASS_ROWS])
        nc.sync.dma_start(w2_w_raw[:], w2_words[0].bitcast(I32))
        tab_w = keep.tile([P, T], I32, tag="table_words", align_bytes=64)
        nc.sync.dma_start(
            tab_w[:], tab_words[0].rearrange("p t i -> p (t i)").bitcast(I32), max_dma_last_dim=TABLE_PIECE_BYTES
        )
        for q in range(QUADRANTS):
            nc.scalar.dma_start(w2_b_raw[32 * q : 32 * q + 4, :].bitcast(I32), w2_scales[0, 4 * q : 4 * q + 4, :].bitcast(I32))
        gain_sb = keep.tile([P, PASSES, PACK], F32)
        nc.sync.dma_start(gain_sb[:], gain.rearrange("(a p t) -> p a t", p=P, t=PACK))
        p4 = load_list(pos4, "p4")
        nc.sync.dma_start(w1_raw[1][:], w1_rows[:, :, PASS_ROWS : 2 * PASS_ROWS])
        w4_w = keep.tile([P, PASSES, N], I32, align_bytes=64)
        nc.sync.dma_start(w4_w[:], w4_words.rearrange("a p c i -> p a (c i)").bitcast(I32))
        for q in range(QUADRANTS):
            nc.sync.dma_start(
                w4_b[32 * q : 32 * q + 4, :].bitcast(I32).rearrange("r (a c) -> r a c", a=PASSES),
                w4_scales[:, 4 * q : 4 * q + 4, :].bitcast(I32).rearrange("a r c -> r a c"),
            )

        v_b = keep.tile([P, S], U8, align_bytes=64)
        width = S // SCALE_GATHERS
        for g in range(SCALE_GATHERS):
            nc.vector.tensor_copy(
                v_b[:, g * width : (g + 1) * width], tab_b[:].indirect(idx[:, entries(g * width, (g + 1) * width)])
            )
        v_w = keep.tile([P, S], U32, tag="scales_then_words", align_bytes=64)

        def gather_words(c):
            nc.vector.tensor_copy(
                v_w[:, c * BANK : (c + 1) * BANK], tab_w[:].bitcast(U32).indirect(idx[:, entries(c * BANK, (c + 1) * BANK)])
            )

        w2_w = keep.tile([P, 2 * H], U8, align_bytes=64)
        w2_w_dealt = w2_w[:].bitcast(U16).rearrange("p (a t m) -> p a t m", a=PASSES, t=PACK)
        w2_w_given = w2_w_raw[:].bitcast(U16).rearrange("p (a m t) -> p a t m", a=PASSES, t=PACK)
        w2_b_given = w2_b_raw[:].rearrange("p (a m t) -> p a t m", a=PASSES, t=PACK)
        w2_b = {}
        w1_bf = {}
        w1_q = {}

        def deal_w2_words(s0, count):
            a, t = divmod(s0, PACK)
            nc.scalar.copy(w2_w_dealt[:, a, t : t + count, :], w2_w_given[:, a, t : t + count, :])

        def deal_w2_scales(s0, count, tag):
            a, t = divmod(s0, PACK)
            dealt = keep.tile([P, count * P], U8, name="w2_b%d" % s0, tag=tag, align_bytes=64)
            nc.gpsimd.tensor_copy(dealt[:].rearrange("p (t m) -> p t m", t=count), w2_b_given[:, a, t : t + count, :])
            for i in range(count):
                w2_b[s0 + i] = dealt[:, i * P : (i + 1) * P]

        def deal_w1(s0, count, tag):
            a, t = divmod(s0, PACK)
            w1_bf[s0] = keep.tile([P, count, P, PACK], BF16, name="w1_bf%d" % s0, tag=tag, align_bytes=64)
            nc.scalar.copy(w1_bf[s0][:], w1_raw[a][:].rearrange("p j (m t) -> p t m j", t=PACK)[:, t : t + count, :, :])

        def mx_tiles(name, columns, tag):
            words = keep.tile([P, columns], U32, name=name + "_w", tag=tag, align_bytes=64)
            scale_bytes = keep.tile([P, columns], U8, name=name + "_b", align_bytes=64)
            return words, scale_bytes

        def quantize(operand, cols, src):
            nc.vector.quantize_mx(out=operand[0][:, cols].bitcast(FP8X4), scales=operand[1][:, cols], in_=src)

        def quantize_w1(s0, count, tag):
            operand = mx_tiles("w1q%d" % s0, count * P, tag)
            quantize(operand, slice(0, count * P), w1_bf[s0][:].rearrange("p t m j -> p (t m j)"))
            for i in range(count):
                w1_q[s0 + i] = (operand[0][:, i * P : (i + 1) * P], operand[1][:, i * P : (i + 1) * P])

        def interleave(engine_copy, dst, src):
            engine_copy(dst.rearrange("p (c i) t -> p c t i", i=4), src.rearrange("p t (c i) -> p c t i", i=4))

        h = {}
        linear_sb = {}
        gained_sb = {}

        def first_products(s, c, arg_bank, linear_bank):
            toks = slice(c * BANK, (c + 1) * BANK)
            arg = psum.tile([P, BANK], F32, name="arg", tag="bank%d" % arg_bank)
            nc.tensor.matmul_mx(
                out=arg[:], lhsT=w2_w[:, 2 * s * P : 2 * (s + 1) * P].bitcast(FP4X4), lhsT_scale=w2_b[s],
                rhs=v_w[:, toks].bitcast(FP8X4), rhs_scale=v_b[:, toks], start=True, stop=True,
            )
            linear = psum.tile([P, BANK], F32, name="linear", tag="bank%d" % linear_bank)
            nc.tensor.matmul_mx(
                out=linear[:], lhsT=w1_q[s][0].bitcast(FP8X4), lhsT_scale=w1_q[s][1],
                rhs=v_w[:, toks].bitcast(FP8X4), rhs_scale=v_b[:, toks], start=True, stop=True,
            )
            return arg, linear

        def gain_column(s):
            a, t = divmod(s, PACK)
            return gain_sb[:, a, t : t + 1]

        def head_chunk(s, c):
            arg, linear = first_products(s, c, s, 2 + 2 * ((c + 2) % 3) + s)
            if (s, c) == (HEAD - 1, CHUNKS - 1):
                th = keep.tile([P, BANK], F32, name="th_last", tag="pair_0", align_bytes=64)
            else:
                th = ring.tile([P, BANK], F32, name="th", tag="quarter", bufs=HEAD * CHUNKS)
            nc.scalar.activation(th[:], arg[:], ACT.Tanh)
            nc.vector.scalar_tensor_tensor(
                out=h[s][:, c * BANK : (c + 1) * BANK], in0=th[:], scalar=gain_column(s), in1=linear[:],
                op0=ALU.mult, op1=ALU.add,
            )

        def first_stage_terms(s):
            tanh_sb = keep.tile([P, S], F32, name="tanh_sb", tag="tanh_first" if s == HEAD else "tanh_later", align_bytes=64)
            linear_sb[s] = ring.tile([P, S], F32, name="linear_sb")
            gained_sb[s] = ring.tile([P, S], F32, name="gained_sb")
            for c in range(CHUNKS):
                toks = slice(c * BANK, (c + 1) * BANK)
                arg, linear = first_products(s, c, 2 * c, 2 * c + 1)
                nc.scalar.activation(tanh_sb[:, toks], arg[:], ACT.Tanh)
                nc.scalar.copy(linear_sb[s][:, toks], linear[:])
            nc.scalar.activation(gained_sb[s][:], tanh_sb[:], ACT.Copy, scale=gain_column(s))

        def add_terms(s):
            h[s] = keep.tile([P, S], F32, name="h", tag="window%d" % (s % WINDOWS))
            nc.gpsimd.tensor_tensor(h[s][:], linear_sb[s][:], gained_sb[s][:], ALU.add)

        w3_q = {}
        a2_q = {}
        scores = {}
        halves = [slice(0, HALF), slice(HALF, KEPT)]

        def second_products(a, u, o):
            cols = slice(o * P, (o + 1) * P)
            if a == 0:
                scores[u, o] = psum.tile([P, 2, HALF], F32, name="scores", tag="bank%d" % (OUT_TILES * u + o))
            nc.tensor.matmul_mx(
                out=scores[u, o][:, 0, :], lhsT=w3_q[a][0][:, cols].bitcast(FP8X4), lhsT_scale=w3_q[a][1][:, cols],
                rhs=a2_q[a][0][:, halves[u]].bitcast(FP8X4), rhs_scale=a2_q[a][1][:, halves[u]],
                start=(a == 0), stop=False,
            )
            nc.tensor.matmul_mx(
                out=scores[u, o][:, 1, :], lhsT=w4_w[:, a, cols].bitcast(FP8X4),
                lhsT_scale=w4_b[:, a * N + o * P : a * N + (o + 1) * P],
                rhs=a2_q[a][0][:, halves[u]].bitcast(FP8X4), rhs_scale=a2_q[a][1][:, halves[u]],
                start=False, stop=(a == PASSES - 1),
            )

        for s0 in (0, HEAD):
            deal_w1(s0, HEAD, "w1_bf%d" % s0)
            deal_w2_words(s0, HEAD)
            deal_w2_scales(s0, HEAD, "w2_b%d" % s0)
            quantize_w1(s0, HEAD, "w1q%d" % s0)
        deal_w2_words(PACK, PACK)
        for c in range(CHUNKS):
            gather_words(c)
        deal_w2_scales(PACK, PACK, "table_words")
        for s in range(HEAD):
            h[s] = keep.tile([P, S], F32, name="h", tag="window%d" % s)
        for c in range(CHUNKS):
            for s in range(HEAD):
                head_chunk(s, c)
        deal_w1(PACK, 1, "w1q0")

        a2_f32 = {}
        last = SLICES - 1
        for s in range(SLICES):
            a, t = divmod(s, PACK)
            if s == 1:
                deal_w1(PACK + 1, PACK - 1, "tanh_first")
            if s + 2 < SLICES:
                first_stage_terms(s + 2)
            if s == last - 1:
                late_bf = keep.tile([P, (PASSES + 1) * N * PACK], BF16, name="late_bf", tag="tanh_later", align_bytes=64)
                w3_bf = [late_bf[:, i * N * PACK : (i + 1) * N * PACK] for i in range(PASSES)]
                a2_first_bf = late_bf[:, PASSES * N * PACK :]
                interleave(nc.scalar.copy, a2_first_bf.rearrange("p (c t) -> p c t", t=PACK), a2_f32[0][:])
                for a3 in range(PASSES):
                    w3_raw = keep.tile([P, PACK, N], F32, name="w3_raw", tag="raw%d" % a3)
                    nc.sync.dma_start(
                        w3_raw[:], w3[PASS_ROWS * a3 : PASS_ROWS * (a3 + 1), :].rearrange("(p j) c -> p j c", j=PACK)
                    )
                    interleave(nc.scalar.copy, w3_bf[a3].rearrange("p (c t) -> p c t", t=PACK), w3_raw[:])
                    w3_q[a3] = mx_tiles("w3q%d" % a3, N, "w3q%d" % a3)
                    quantize(w3_q[a3], slice(0, N), w3_bf[a3])

            pair_tag = {1: "pair_1", 2: "pair_2", last: "pair_2"}.get(s, "pair_0")
            pair = keep.tile([P, 2 * PAIRS], F32, name="pair", tag=pair_tag, align_bytes=64)
            nc.vector.tensor_copy(pair[:, 0:PAIRS], h[s][:].indirect(p1[:]))
            nc.vector.tensor_copy(pair[:, PAIRS:], h[s][:].indirect(p2[:]))
            cut = HALF if s == last else KEPT - SPACER
            parts = [slice(0, cut), slice(cut, KEPT)]
            part_entries = [entries(0, cut), entries(cut, KEPT)]
            deposit = keep.tile([P, KEPT], F32, name="deposit", tag="pair_1" if s == 0 else "deposit", align_bytes=64)
            nc.vector.tensor_copy(deposit[:, parts[0]], h[s][:].indirect(p4[:, part_entries[0]]))
            a1 = keep.tile([P, PAIRS], F32, name="a1", tag="window%d" % ((s + 2) % WINDOWS))
            nc.vector.tensor_tensor(a1[:], pair[:, 0:PAIRS], pair[:, PAIRS:], ALU.max)
            if s == 1:
                quantize_w1(PACK, 1, pair_tag)
            if s == 2:
                quantize_w1(PACK + 1, PACK - 1, pair_tag)
            if s == last:
                a2_q[0] = mx_tiles("a2q0", KEPT, pair_tag)
                quantize(a2_q[0], slice(0, KEPT), a2_first_bf)
                for u in range(2):
                    for o in range(OUT_TILES):
                        second_products(0, u, o)
            if t == 0:
                a2_f32[a] = ring.tile([P, PACK, KEPT], F32, name="a2_f32")

            def product(part):
                nc.vector.tensor_tensor(
                    a2_f32[a][:, t, parts[part]], a1[:].indirect(p3[:, part_entries[part]]), deposit[:, parts[part]], ALU.mult
                )

            if s == last:
                product(0)
            nc.vector.tensor_copy(deposit[:, parts[1]], h[s][:].indirect(p4[:, part_entries[1]]))
            if s < last:
                product(0)
            product(1)
            if s + 2 < SLICES:
                add_terms(s + 2)

        a2_q[1] = mx_tiles("a2q1", KEPT, "a2q1")
        for u, engine_copy in enumerate((nc.scalar.copy, nc.vector.tensor_copy)):
            a2_half_bf = ring.tile([P, HALF, PACK], BF16, name="a2_half_bf", align_bytes=64)
            interleave(engine_copy, a2_half_bf[:], a2_f32[1][:, :, halves[u]])
            quantize(a2_q[1], halves[u], a2_half_bf[:].rearrange("p c t -> p (c t)"))
            for o in range(OUT_TILES):
                second_products(1, u, o)
        for u in range(2):
            for o in range(OUT_TILES):
                bounded = ring.tile([P, HALF], F32, name="bounded", bufs=OUT_TILES)
                nc.scalar.activation(bounded[:], scores[u, o][:, 0, :], ACT.Tanh)
                result = ring.tile([P, HALF], F32, name="result", tag="quarter", bufs=HEAD * CHUNKS)
                nc.vector.tensor_tensor(result[:], scores[u, o][:, 1, :], bounded[:], ALU.max)
                nc.sync.dma_start(out[o * P : (o + 1) * P, halves[u]], result[:])
